import numpy as np
import ml_dtypes


def mxq(x, axis, fmt="e4m3"):
    dtype, down = {"e4m3": (ml_dtypes.float8_e4m3fn, 7), "e5m2": (ml_dtypes.float8_e5m2, 14)}[fmt]
    v = np.moveaxis(np.asarray(x, np.float32).astype(ml_dtypes.bfloat16).astype(np.float64), axis, -1)
    blocks = v.reshape(v.shape[:-1] + (-1, 32))
    amax = np.abs(blocks).max(-1, keepdims=True)
    byte = np.maximum(np.where(amax > 0, np.frexp(amax)[1] - 1 + 127, 0) - down, 1)
    scale = np.exp2(byte - 127.0)
    codes = (blocks / scale).astype(np.float32).astype(dtype).astype(np.float64)
    return np.moveaxis((codes * scale).reshape(v.shape), -1, axis)


WIDE = False


def mx_kscale(k):
    if not WIDE:
        return np.ones(k)
    levels = np.array([10, -10, 5, -5, 0])
    if k % 512:
        return np.exp2(np.random.permutation(np.resize(levels, k // 32))).repeat(32)
    a = np.empty((k // 512, 16))
    for p in range(k // 512):
        a[p, :8] = np.random.permutation(np.resize(levels, 8))
        for g in range(8):
            far = levels[np.abs(levels - a[p, g]) >= 10]
            a[p, g + 8] = far[np.random.randint(len(far))]
    return np.exp2(a.ravel()).repeat(32)


def f64(x):
    return np.asarray(x).astype(np.float64)


def striped(idx):
    return np.tile(idx.reshape(-1, 16).T, (8, 1)).astype(np.uint16)


def unstriped(offs):
    return offs[:16].T.reshape(-1).astype(np.int64)


E2M1 = np.array([0.0, 0.5, 1.0, 1.5, 2.0, 3.0, 4.0, 6.0, -0.0, -0.5, -1.0, -1.5, -2.0, -3.0, -4.0, -6.0])


def pack_weight(w, fmt):
    k, n = w.shape
    w = f64(np.asarray(w, np.float32).astype(ml_dtypes.bfloat16)).reshape(k // 32, 32, n)
    amax = np.abs(w).max(1)
    if fmt == "e4m3":
        byte = np.frexp(amax)[1] - 1 + 127 - 7
    else:
        mant, ex = np.frexp(amax / 6.0)
        byte = np.where(mant > 0.5, ex, ex - 1) + 127
    byte = np.clip(np.where(amax > 0, byte, 1), 1, 254)
    scaled = (w * np.exp2(127.0 - byte)[:, None, :]).reshape(k, n).astype(np.float32)
    by_word = np.ascontiguousarray(scaled.reshape(k // 512, 128, 4, n).transpose(0, 1, 3, 2))
    if fmt == "e4m3":
        words = by_word.astype(ml_dtypes.float8_e4m3fn).view(np.uint8)
    else:
        c = by_word.astype(ml_dtypes.float4_e2m1fn).view(np.uint8) & 0xF
        words = (c[..., 0::2] | (c[..., 1::2] << 4)).reshape(k // 512, 128, 2 * n)
    return np.ascontiguousarray(words), np.ascontiguousarray(byte.astype(np.uint8).reshape(k // 512, 16, n))


def unpack_weight(words, scales, fmt):
    g, _, n = scales.shape
    words = np.ascontiguousarray(words).reshape(g, 128, n, -1)
    if fmt == "e4m3":
        vals = words.view(ml_dtypes.float8_e4m3fn).astype(np.float64)
    else:
        nib = np.empty((g, 128, n, 4), np.uint8)
        nib[..., 0::2] = words & 0xF
        nib[..., 1::2] = words >> 4
        vals = E2M1[nib]
    vals = vals * np.repeat(np.exp2(scales.astype(np.float64) - 127.0), 8, axis=1)[..., None]
    return vals.transpose(0, 1, 3, 2).reshape(g * 512, n)


K, T, E1, C1, E2, C2, H = 256, 768, 3, 256, 6, 128, 512
N = 512


def by_expert(wq, xq, E, C):
    return np.concatenate([wq[e].T @ xq[:, e * C:(e + 1) * C] for e in range(E)], axis=1)


def setup_inputs():
    n = np.random.standard_normal
    v = mx_kscale(N)
    u = mx_kscale(H)
    slots1, slots2 = np.random.permutation(T), np.random.permutation(T)
    dy = pack_weight(n((N, T)) * v[:, None], "e4m3")
    w2t = [pack_weight(m, "e4m3") for m in n((E2, N, H)) / np.sqrt(N) / v[None, :, None] * u]
    w1t = [pack_weight(m, "e2m1") for m in n((E1, H, K)) / np.sqrt(H) / u[None, :, None]]
    return {
        "dy_words": dy[0],
        "dy_scales": dy[1],
        "w2t_words": np.stack([m[0] for m in w2t]),
        "w2t_scales": np.stack([m[1] for m in w2t]),
        "w1t_words": np.stack([m[0] for m in w1t]),
        "w1t_scales": np.stack([m[1] for m in w1t]),
        "gate1": (np.tile(np.random.uniform(0.2, 1.0, T), (128, 1))).astype(np.float32),
        "gate2": (np.tile(np.random.uniform(0.2, 1.0, T), (128, 1))).astype(np.float32),
        "offs": striped(slots1),
        "offs2": striped(slots2),
    }


def reference(dy_words, dy_scales, w2t_words, w2t_scales, w1t_words, w1t_scales, gate1, gate2, offs, offs2):
    w2t = np.stack([unpack_weight(w2t_words[e], w2t_scales[e], "e4m3") for e in range(E2)])
    w1t = np.stack([unpack_weight(w1t_words[e], w1t_scales[e], "e2m1") for e in range(E1)])
    idx, idx2 = unstriped(offs), unstriped(offs2)
    gq = unpack_weight(dy_words, dy_scales, "e4m3")[:, idx2]
    dc = np.zeros((H, T))
    dc[:, idx2] = f64(gate2[:1]) * by_expert(w2t, gq, E2, C2)
    da = f64(gate1[:1]) * dc[:, idx]
    out = np.zeros((K, T))
    out[:, idx] = by_expert(w1t, mxq(da, 0, "e4m3"), E1, C1)
    return out

@@ -1,0 +1,217 @@
+from contextlib import ExitStack
+
+import concourse.mybir as mybir
+from concourse.masks import make_identity
+
+K, T, H, N = 256, 768, 512, 512
+E1, C1, E2, C2 = 3, 256, 6, 128
+FLOPS = 2 * T * (N * H + H * K)
+
+F32 = mybir.dt.float32
+BF16 = mybir.dt.bfloat16
+I32 = mybir.dt.int32
+U32 = mybir.dt.uint32
+U16 = mybir.dt.uint16
+U8 = mybir.dt.uint8
+FP8X4 = mybir.dt.float8_e4m3fn_x4
+FP4X4 = mybir.dt.float4_e2m1fn_x4
+COPY = mybir.ActivationFunctionType.Copy
+MULT = mybir.AluOpType.mult
+
+P = 128
+LIST = 16
+HP = H // P
+KP = K // P
+BLOCKS = T // P
+GROUPS = ((0, 1), (1, 3), (3, 6))
+
+
+def entries(offsets, first, last):
+    return offsets[:, first // LIST : last // LIST]
+
+
+def load_scale_rows(nc, plane, rows):
+    for r in range(4):
+        nc.sync.dma_start(out=plane[r:P:32].bitcast(I32), in_=rows[r].bitcast(I32))
+
+
+def tile_moe_seb_none_kernel(
+    tc, dy_words, dy_scales, w2t_words, w2t_scales, w1t_words, w1t_scales, gate1, gate2, offs, offs2, out
+):
+    nc = tc.nc
+    with ExitStack() as ctx:
+        held = ctx.enter_context(tc.tile_pool(name="held", bufs=1))
+        psum = ctx.enter_context(tc.psum_pool(name="psum", bufs=2))
+
+        list2 = held.tile([P, T // LIST], U16, name="list2")
+        list1 = held.tile([P, T // LIST], U16, name="list1")
+        dy_w = held.tile([P, T], U32, name="dy_w", align_bytes=64)
+        dy_s = held.tile([P, T], U8, name="dy_s", align_bytes=64)
+        w2_s = held.tile([P, E2, H], U8, name="w2_s", align_bytes=64)
+        w1_s = held.tile([P, E1, K], U8, name="w1_s", align_bytes=64)
+        q_rows = held.tile([P, T], F32, name="q_rows")
+        identity = held.tile([P, P], F32, name="identity")
+
+        nc.gpsimd.memset(w2_s[:].bitcast(I32), 0)
+        nc.vector.memset(w1_s[:].bitcast(I32), 0)
+
+        w2_w = {}
+
+        def load_w2_words(f0, f1):
+            tile = held.tile([P, f1 - f0, H], U32, name=f"w2_w{f0}", tag="weights", bufs=2, align_bytes=64)
+            src = w2t_words[f0:f1, 0].rearrange("f p i d -> p f (i d)")
+            nc.sync.dma_start(out=tile[:].bitcast(I32), in_=src.bitcast(I32))
+            for f in range(f0, f1):
+                w2_w[f] = tile[:, f - f0, :]
+
+        nc.sync.dma_start(out=dy_w[:].bitcast(I32), in_=dy_words[0].rearrange("p t d -> p (t d)").bitcast(I32))
+        nc.sync.dma_start(list2[:], offs2)
+        for q in range(4):
+            rows = dy_scales[0, 4 * q : 4 * q + 4, :].bitcast(I32)
+            nc.sync.dma_start(
+                out=dy_s[32 * q : 32 * q + 32, :].bitcast(I32), in_=rows.unsqueeze(0).to_broadcast([8, 4, T // 4])
+            )
+        load_w2_words(*GROUPS[0])
+        load_scale_rows(nc, w2_s, w2t_scales[:, 0].rearrange("f (q r) i -> r q f i", r=4))
+        nc.sync.dma_start(out=q_rows[:], in_=gate2)
+        load_w2_words(*GROUPS[1])
+        nc.sync.dma_start(list1[:], offs)
+        load_scale_rows(nc, w1_s, w1t_scales[:, 0].rearrange("e (q r) k -> r q e k", r=4))
+        make_identity(nc, identity[:])
+
+        slot_w, slot_s = {}, {}
+        for first, last in ((0, 256), (256, T)):
+            for table, dtype, by_expert, name in ((dy_w, U32, slot_w, "slot_w"), (dy_s, U8, slot_s, "slot_s")):
+                tile = held.tile([P, last - first], dtype, name=f"{name}{first}", tag=f"{name}{first}", align_bytes=64)
+                nc.vector.tensor_copy(tile[:], table[:].indirect(entries(list2, first, last)))
+                for f in range(first // C2, last // C2):
+                    by_expert[f] = tile[:, f * C2 - first : (f + 1) * C2 - first]
+
+        sums = [held.tile([P, HP, (f1 - f0) * C2], F32, name=f"sums{f0}") for f0, f1 in GROUPS]
+
+        def multiply_w2(f, s, acc):
+            cols = slice(s * P, (s + 1) * P)
+            nc.tensor.matmul_mx(
+                out=acc,
+                lhsT=w2_w[f][:, cols].bitcast(FP8X4),
+                lhsT_scale=w2_s[:, f, cols],
+                rhs=slot_w[f].bitcast(FP8X4),
+                rhs_scale=slot_s[f],
+                start=True,
+                stop=True,
+            )
+
+        for s, tag in enumerate(("acc2", "turned", "back", "acc1")):
+            acc = psum.tile([P, C2], F32, name=f"first{s}", tag=tag)
+            multiply_w2(0, s, acc[:])
+            nc.scalar.activation(sums[0][:, s, :], acc[:], COPY)
+        for c, (f0, f1) in list(enumerate(GROUPS))[1:]:
+            if c == 2:
+                load_w2_words(f0, f1)
+            for f in range(f0, f1):
+                acc = psum.tile([P, HP, C2], F32, name="acc2", tag="acc2")
+                for s in range(HP):
+                    multiply_w2(f, s, acc[:, s, :])
+                nc.scalar.activation(sums[c][:, :, (f - f0) * C2 : (f - f0 + 1) * C2], acc[:], COPY)
+
+        w1_w = held.tile([P, E1, 2 * K], U8, name="w1_w", tag="weights", bufs=2, align_bytes=64)
+        nc.sync.dma_start(out=w1_w[:].bitcast(I32), in_=w1t_words[:, 0].rearrange("e p c -> p e c").bitcast(I32))
+        g_cols = held.tile([P, BLOCKS], F32, name="g_cols", tag="slot_s0", align_bytes=64)
+        with nc.allow_non_contiguous_dma(reason="one gate value to a partition"):
+            nc.sync.dma_start(out=g_cols[:], in_=gate1[0].rearrange("(b p) -> p b", p=P))
+
+        dc = [held.tile([P, T], F32, name=f"dc{s}") for s in range(HP)]
+
+        def scatter_dc(c, s):
+            first, last = GROUPS[c][0] * C2, GROUPS[c][1] * C2
+            nc.vector.tensor_tensor(
+                dc[s][:].indirect(entries(list2, first, last)), sums[c][:, s, :], q_rows[:, first:last], MULT
+            )
+
+        picked = {}
+
+        def gather_tile(b0, b1, tag):
+            tile = held.tile([P, HP, (b1 - b0) * P], F32, name=f"picked{b0}", tag=tag, align_bytes=64)
+            for b in range(b0, b1):
+                picked[b] = tile[:, :, (b - b0) * P : (b - b0 + 1) * P]
+            return tile
+
+        def gather_dc(tile, b0, b1, s):
+            nc.vector.tensor_copy(tile[:, s, :], dc[s][:].indirect(entries(list1, b0 * P, b1 * P)))
+
+        da_words, codes, code_s, results = {}, {}, {}, {}
+
+        def weigh_and_turn(b):
+            turned = psum.tile([P, HP, P], F32, name="turned", tag="turned")
+            for s in range(HP):
+                nc.tensor.transpose(turned[:, s, :], picked[b][:, s, :], identity[:])
+            da_rows = held.tile([P, 2, P, 2], BF16, name=f"da_rows{b}", align_bytes=64)
+            nc.scalar.activation(
+                da_rows[:],
+                turned[:].rearrange("j s q -> j (s q)").rearrange("j (p u e) -> j u p e", u=2, e=2),
+                COPY,
+                scale=g_cols[:, b : b + 1],
+            )
+            back = psum.tile([P, 2, P], F32, name="back", tag="back")
+            pairs = da_rows[:].rearrange("j u p e -> j u (p e)").bitcast(F32)
+            for u in range(2):
+                nc.tensor.transpose(back[:, u, :], pairs[:, u, :], identity[:])
+            da_words[b] = held.tile([P, 4 * P], BF16, name=f"da_words{b}", tag=f"da_words{b}", align_bytes=64)
+            nc.scalar.copy(
+                da_words[b][:].bitcast(F32).rearrange("p (j u) -> p j u", u=2),
+                back[:].rearrange("p u j -> p j u"),
+            )
+
+        def quantise_and_multiply(b):
+            codes[b] = held.tile([P, P], U32, name=f"codes{b}", align_bytes=64)
+            code_s[b] = held.tile([P, P], U8, name=f"code_s{b}", align_bytes=64)
+            nc.vector.quantize_mx(out=codes[b][:].bitcast(FP8X4), scales=code_s[b][:], in_=da_words[b][:])
+            e = b * P // C1
+            acc = psum.tile([P, KP, P], F32, name="acc1", tag="acc1")
+            for h in range(KP):
+                nc.tensor.matmul_mx(
+                    out=acc[:, h, :],
+                    lhsT=w1_w[:, e, 2 * P * h : 2 * P * (h + 1)].bitcast(FP4X4),
+                    lhsT_scale=w1_s[:, e, h * P : (h + 1) * P],
+                    rhs=codes[b][:].bitcast(FP8X4),
+                    rhs_scale=code_s[b][:],
+                    start=True,
+                    stop=True,
+                )
+            results[b] = held.tile([P, KP, P], F32, name=f"results{b}")
+            nc.scalar.activation(results[b][:], acc[:], COPY)
+
+        dx = [held.tile([P, T], F32, name=f"dx{h}") for h in range(KP)]
+
+        def scatter_dx(b):
+            for h in range(KP):
+                nc.vector.tensor_copy(dx[h][:].indirect(entries(list1, b * P, (b + 1) * P)), results[b][:, h, :])
+
+        for c in range(2):
+            for s in range(HP):
+                scatter_dc(c, s)
+        first_tile = gather_tile(0, 1, "picked0")
+        scatter_dc(2, 0)
+        for s in range(1, HP):
+            scatter_dc(2, s)
+            gather_dc(first_tile, 0, 1, s - 1)
+        gather_dc(first_tile, 0, 1, HP - 1)
+        weigh_and_turn(0)
+        for b0, b1 in ((1, 2), (2, 4)):
+            tile = gather_tile(b0, b1, f"picked{b0}")
+            for s in range(HP):
+                gather_dc(tile, b0, b1, s)
+        weigh_and_turn(1)
+        quantise_and_multiply(0)
+        tile = gather_tile(4, 6, "da_words0")
+        for s in range(HP):
+            gather_dc(tile, 4, 6, s)
+        for b in range(1, BLOCKS):
+            if b + 1 < BLOCKS:
+                weigh_and_turn(b + 1)
+            quantise_and_multiply(b)
+            scatter_dx(b - 1)
+        scatter_dx(BLOCKS - 1)
+
+        for h in range(KP):
+            nc.sync.dma_start(out=out[h * P : (h + 1) * P, :], in_=dx[h][:])

@@ -24,6 +24,7 @@ HP = H // P
 KP = K // P
 BLOCKS = T // P
 GROUPS = ((0, 1), (1, 3), (3, 6))
+WINDOW = 1024
 
 
 def entries(offsets, first, last):
@@ -45,15 +46,25 @@ def tile_moe_seb_none_kernel(
 
         list2 = held.tile([P, T // LIST], U16, name="list2")
         list1 = held.tile([P, T // LIST], U16, name="list1")
-        dy_w = held.tile([P, T], U32, name="dy_w", align_bytes=64)
-        dy_s = held.tile([P, T], U8, name="dy_s", align_bytes=64)
-        w2_s = held.tile([P, E2, H], U8, name="w2_s", align_bytes=64)
+        dy_w = held.tile([P, WINDOW], U32, name="dy_w", align_bytes=64)
+        dy_s = held.tile([P, WINDOW], U8, name="dy_s", align_bytes=64)
+        w2_s = [held.tile([P, H], U8, name=f"w2_s{a}", align_bytes=64) for a in range(2)]
         w1_s = held.tile([P, E1, K], U8, name="w1_s", align_bytes=64)
-        q_rows = held.tile([P, T], F32, name="q_rows")
+        q_rows = [held.tile([P, (f1 - f0) * C2], F32, name=f"q_rows{f0}") for f0, f1 in GROUPS]
         identity = held.tile([P, P], F32, name="identity")
 
-        nc.gpsimd.memset(w2_s[:].bitcast(I32), 0)
+        nc.vector.memset(w2_s[0][:].bitcast(I32), 0)
+        nc.vector.memset(dy_s[:, T:].bitcast(I32), 0)
+        nc.vector.memset(dy_w[:, T:].bitcast(I32), 0)
+        nc.vector.memset(w2_s[1][:].bitcast(I32), 0)
         nc.vector.memset(w1_s[:].bitcast(I32), 0)
+
+        def load_w2_scales(f0, f1):
+            for q in range(4):
+                nc.sync.dma_start(
+                    out=w2_s[f0 // 4][32 * q : 32 * q + 4 * (f1 - f0), :].bitcast(I32),
+                    in_=w2t_scales[f0:f1, 0, 4 * q : 4 * q + 4, :].bitcast(I32),
+                )
 
         w2_w = {}
 
@@ -64,28 +75,34 @@ def tile_moe_seb_none_kernel(
             for f in range(f0, f1):
                 w2_w[f] = tile[:, f - f0, :]
 
-        nc.sync.dma_start(out=dy_w[:].bitcast(I32), in_=dy_words[0].rearrange("p t d -> p (t d)").bitcast(I32))
         nc.sync.dma_start(list2[:], offs2)
         for q in range(4):
             rows = dy_scales[0, 4 * q : 4 * q + 4, :].bitcast(I32)
-            nc.sync.dma_start(
-                out=dy_s[32 * q : 32 * q + 32, :].bitcast(I32), in_=rows.unsqueeze(0).to_broadcast([8, 4, T // 4])
+            (nc.sync, nc.scalar)[q // 2].dma_start(
+                out=dy_s[32 * q : 32 * q + 32, :T].bitcast(I32), in_=rows.unsqueeze(0).to_broadcast([8, 4, T // 4])
             )
+        nc.sync.dma_start(out=dy_w[:, :T].bitcast(I32), in_=dy_words[0].rearrange("p t d -> p (t d)").bitcast(I32))
         load_w2_words(*GROUPS[0])
-        load_scale_rows(nc, w2_s, w2t_scales[:, 0].rearrange("f (q r) i -> r q f i", r=4))
-        nc.sync.dma_start(out=q_rows[:], in_=gate2)
+        load_w2_scales(0, 4)
+        nc.sync.dma_start(out=q_rows[0][:], in_=gate2[:, : GROUPS[0][1] * C2])
         load_w2_words(*GROUPS[1])
+        for c in (1, 2):
+            nc.sync.dma_start(out=q_rows[c][:], in_=gate2[:, GROUPS[c][0] * C2 : GROUPS[c][1] * C2])
+        load_w2_scales(4, E2)
         nc.sync.dma_start(list1[:], offs)
         load_scale_rows(nc, w1_s, w1t_scales[:, 0].rearrange("e (q r) k -> r q e k", r=4))
         make_identity(nc, identity[:])
 
         slot_w, slot_s = {}, {}
-        for first, last in ((0, 256), (256, T)):
-            for table, dtype, by_expert, name in ((dy_w, U32, slot_w, "slot_w"), (dy_s, U8, slot_s, "slot_s")):
-                tile = held.tile([P, last - first], dtype, name=f"{name}{first}", tag=f"{name}{first}", align_bytes=64)
-                nc.vector.tensor_copy(tile[:], table[:].indirect(entries(list2, first, last)))
-                for f in range(first // C2, last // C2):
-                    by_expert[f] = tile[:, f * C2 - first : (f + 1) * C2 - first]
+        for table, dtype, by_expert, name, first, last in (
+            (dy_s, U8, slot_s, "slot_s", 0, T),
+            (dy_w, U32, slot_w, "slot_w", 0, C2),
+            (dy_w, U32, slot_w, "slot_w", C2, T),
+        ):
+            tile = held.tile([P, last - first], dtype, name=f"{name}{first}", tag=f"{name}{first}", align_bytes=64)
+            nc.vector.tensor_copy(tile[:], table[:].indirect(entries(list2, first, last)))
+            for f in range(first // C2, last // C2):
+                by_expert[f] = tile[:, f * C2 - first : (f + 1) * C2 - first]
 
         sums = [held.tile([P, HP, (f1 - f0) * C2], F32, name=f"sums{f0}") for f0, f1 in GROUPS]
 
@@ -94,7 +111,7 @@ def tile_moe_seb_none_kernel(
             nc.tensor.matmul_mx(
                 out=acc,
                 lhsT=w2_w[f][:, cols].bitcast(FP8X4),
-                lhsT_scale=w2_s[:, f, cols],
+                lhsT_scale=w2_s[f // 4][4 * (f % 4) :, cols],
                 rhs=slot_w[f].bitcast(FP8X4),
                 rhs_scale=slot_s[f],
                 start=True,
@@ -125,7 +142,7 @@ def tile_moe_seb_none_kernel(
         def scatter_dc(c, s):
             first, last = GROUPS[c][0] * C2, GROUPS[c][1] * C2
             nc.vector.tensor_tensor(
-                dc[s][:].indirect(entries(list2, first, last)), sums[c][:, s, :], q_rows[:, first:last], MULT
+                dc[s][:].indirect(entries(list2, first, last)), sums[c][:, s, :], q_rows[c][:], MULT
             )
 
         picked = {}

@@ -42,7 +42,7 @@ def tile_moe_seb_none_kernel(
     nc = tc.nc
     with ExitStack() as ctx:
         held = ctx.enter_context(tc.tile_pool(name="held", bufs=1))
-        psum = ctx.enter_context(tc.psum_pool(name="psum", bufs=2))
+        psum = ctx.enter_context(tc.psum_pool(name="psum", bufs=1))
 
         list2 = held.tile([P, T // LIST], U16, name="list2")
         list1 = held.tile([P, T // LIST], U16, name="list1")
@@ -50,7 +50,7 @@ def tile_moe_seb_none_kernel(
         dy_s = held.tile([P, WINDOW], U8, name="dy_s", align_bytes=64)
         w2_s = [held.tile([P, H], U8, name=f"w2_s{a}", align_bytes=64) for a in range(2)]
         w1_s = held.tile([P, E1, K], U8, name="w1_s", align_bytes=64)
-        q_rows = [held.tile([P, (f1 - f0) * C2], F32, name=f"q_rows{f0}") for f0, f1 in GROUPS]
+        q_rows = [held.tile([P, (f1 - f0) * C2], F32, name=f"q_rows{f0}", tag=f"q_rows{f0}", align_bytes=64) for f0, f1 in GROUPS]
         identity = held.tile([P, P], F32, name="identity")
 
         nc.vector.memset(w2_s[0][:].bitcast(I32), 0)
@@ -104,7 +104,7 @@ def tile_moe_seb_none_kernel(
             for f in range(first // C2, last // C2):
                 by_expert[f] = tile[:, f * C2 - first : (f + 1) * C2 - first]
 
-        sums = [held.tile([P, HP, (f1 - f0) * C2], F32, name=f"sums{f0}") for f0, f1 in GROUPS]
+        sums = [held.tile([P, HP, (f1 - f0) * C2], F32, name=f"sums{f0}", tag=f"sums{f0}", align_bytes=64) for f0, f1 in GROUPS]
 
         def multiply_w2(f, s, acc):
             cols = slice(s * P, (s + 1) * P)
@@ -118,15 +118,15 @@ def tile_moe_seb_none_kernel(
                 stop=True,
             )
 
-        for s, tag in enumerate(("acc2", "turned", "back", "acc1")):
-            acc = psum.tile([P, C2], F32, name=f"first{s}", tag=tag)
+        for s in range(HP):
+            acc = psum.tile([P, C2], F32, name=f"first{s}", tag=f"bank{s}")
             multiply_w2(0, s, acc[:])
             nc.scalar.activation(sums[0][:, s, :], acc[:], COPY)
         for c, (f0, f1) in list(enumerate(GROUPS))[1:]:
             if c == 2:
                 load_w2_words(f0, f1)
             for f in range(f0, f1):
-                acc = psum.tile([P, HP, C2], F32, name="acc2", tag="acc2")
+                acc = psum.tile([P, HP, C2], F32, name="acc2", tag=f"bank{4 + f % 4}")
                 for s in range(HP):
                     multiply_w2(f, s, acc[:, s, :])
                 nc.scalar.activation(sums[c][:, :, (f - f0) * C2 : (f - f0 + 1) * C2], acc[:], COPY)
@@ -147,29 +147,28 @@ def tile_moe_seb_none_kernel(
 
         picked = {}
 
-        def gather_tile(b0, b1, tag):
-            tile = held.tile([P, HP, (b1 - b0) * P], F32, name=f"picked{b0}", tag=tag, align_bytes=64)
-            for b in range(b0, b1):
-                picked[b] = tile[:, :, (b - b0) * P : (b - b0 + 1) * P]
-            return tile
-
-        def gather_dc(tile, b0, b1, s):
-            nc.vector.tensor_copy(tile[:, s, :], dc[s][:].indirect(entries(list1, b0 * P, b1 * P)))
+        def gather_dc(b0, b1, planes, tag=None):
+            name = f"picked{b0}_{planes[0]}"
+            tile = held.tile([P, len(planes), (b1 - b0) * P], F32, name=name, tag=tag or name, align_bytes=64)
+            for place, s in enumerate(planes):
+                nc.vector.tensor_copy(tile[:, place, :], dc[s][:].indirect(entries(list1, b0 * P, b1 * P)))
+                for b in range(b0, b1):
+                    picked[b, s] = tile[:, place, (b - b0) * P : (b - b0 + 1) * P]
 
         da_words, codes, code_s, results = {}, {}, {}, {}
 
         def weigh_and_turn(b):
-            turned = psum.tile([P, HP, P], F32, name="turned", tag="turned")
+            turned = psum.tile([P, HP, P], F32, name="turned", tag=f"bank{(0, 0, 1, 2, 3, 4)[b]}")
             for s in range(HP):
-                nc.tensor.transpose(turned[:, s, :], picked[b][:, s, :], identity[:])
-            da_rows = held.tile([P, 2, P, 2], BF16, name=f"da_rows{b}", align_bytes=64)
+                nc.tensor.transpose(turned[:, s, :], picked[b, s], identity[:])
+            da_rows = held.tile([P, 2, P, 2], BF16, name=f"da_rows{b}", tag=f"rows{b}", align_bytes=64)
             nc.scalar.activation(
                 da_rows[:],
                 turned[:].rearrange("j s q -> j (s q)").rearrange("j (p u e) -> j u p e", u=2, e=2),
                 COPY,
                 scale=g_cols[:, b : b + 1],
             )
-            back = psum.tile([P, 2, P], F32, name="back", tag="back")
+            back = psum.tile([P, 2, P], F32, name="back", tag=f"bank{(1, 2, 3, 4, 5, 6)[b]}")
             pairs = da_rows[:].rearrange("j u p e -> j u (p e)").bitcast(F32)
             for u in range(2):
                 nc.tensor.transpose(back[:, u, :], pairs[:, u, :], identity[:])
@@ -184,7 +183,7 @@ def tile_moe_seb_none_kernel(
             code_s[b] = held.tile([P, P], U8, name=f"code_s{b}", align_bytes=64)
             nc.vector.quantize_mx(out=codes[b][:].bitcast(FP8X4), scales=code_s[b][:], in_=da_words[b][:])
             e = b * P // C1
-            acc = psum.tile([P, KP, P], F32, name="acc1", tag="acc1")
+            acc = psum.tile([P, KP, P], F32, name="acc1", tag=f"bank{(0, 1, 2, 3, 4, 7)[b]}")
             for h in range(KP):
                 nc.tensor.matmul_mx(
                     out=acc[:, h, :],
@@ -195,7 +194,7 @@ def tile_moe_seb_none_kernel(
                     start=True,
                     stop=True,
                 )
-            results[b] = held.tile([P, KP, P], F32, name=f"results{b}")
+            results[b] = held.tile([P, KP, P], F32, name=f"results{b}", align_bytes=64)
             nc.scalar.activation(results[b][:], acc[:], COPY)
 
         dx = [held.tile([P, T], F32, name=f"dx{h}") for h in range(KP)]
@@ -207,22 +206,17 @@ def tile_moe_seb_none_kernel(
         for c in range(2):
             for s in range(HP):
                 scatter_dc(c, s)
-        first_tile = gather_tile(0, 1, "picked0")
         scatter_dc(2, 0)
         for s in range(1, HP):
             scatter_dc(2, s)
-            gather_dc(first_tile, 0, 1, s - 1)
-        gather_dc(first_tile, 0, 1, HP - 1)
+            gather_dc(0, 1, [s - 1])
+        gather_dc(0, 1, [HP - 1])
         weigh_and_turn(0)
-        for b0, b1 in ((1, 2), (2, 4)):
-            tile = gather_tile(b0, b1, f"picked{b0}")
-            for s in range(HP):
-                gather_dc(tile, b0, b1, s)
+        gather_dc(1, 2, range(HP), "q_rows3")
         weigh_and_turn(1)
+        gather_dc(2, 4, range(HP), "sums3")
         quantise_and_multiply(0)
-        tile = gather_tile(4, 6, "da_words0")
-        for s in range(HP):
-            gather_dc(tile, 4, 6, s)
+        gather_dc(4, 6, range(HP), "q_rows3")
         for b in range(1, BLOCKS):
             if b + 1 < BLOCKS:
                 weigh_and_turn(b + 1)

@@ -20,20 +20,14 @@ MULT = mybir.AluOpType.mult
 
 P = 128
 LIST = 16
-HP = H // P
+PACK = 4
 KP = K // P
-BLOCKS = T // P
-GROUPS = ((0, 1), (1, 3), (3, 6))
+GROUPS = ((0, 1), (1, 2), (2, 4), (4, 6))
 WINDOW = 1024
 
 
 def entries(offsets, first, last):
     return offsets[:, first // LIST : last // LIST]
-
-
-def load_scale_rows(nc, plane, rows):
-    for r in range(4):
-        nc.sync.dma_start(out=plane[r:P:32].bitcast(I32), in_=rows[r].bitcast(I32))
 
 
 def tile_moe_seb_none_kernel(
@@ -50,7 +44,8 @@ def tile_moe_seb_none_kernel(
         dy_s = held.tile([P, WINDOW], U8, name="dy_s", align_bytes=64)
         w2_s = [held.tile([P, H], U8, name=f"w2_s{a}", align_bytes=64) for a in range(2)]
         w1_s = held.tile([P, E1, K], U8, name="w1_s", align_bytes=64)
-        q_rows = [held.tile([P, (f1 - f0) * C2], F32, name=f"q_rows{f0}", tag=f"q_rows{f0}", align_bytes=64) for f0, f1 in GROUPS]
+        q_loaded = held.tile([P, E2], F32, name="q_loaded")
+        q_cols = held.tile([P, E2], F32, name="q_cols")
         identity = held.tile([P, P], F32, name="identity")
 
         nc.vector.memset(w2_s[0][:].bitcast(I32), 0)
@@ -84,13 +79,15 @@ def tile_moe_seb_none_kernel(
         nc.sync.dma_start(out=dy_w[:, :T].bitcast(I32), in_=dy_words[0].rearrange("p t d -> p (t d)").bitcast(I32))
         load_w2_words(*GROUPS[0])
         load_w2_scales(0, 4)
-        nc.sync.dma_start(out=q_rows[0][:], in_=gate2[:, : GROUPS[0][1] * C2])
-        load_w2_words(*GROUPS[1])
-        for c in (1, 2):
-            nc.sync.dma_start(out=q_rows[c][:], in_=gate2[:, GROUPS[c][0] * C2 : GROUPS[c][1] * C2])
+        with nc.allow_non_contiguous_dma(reason="one gate value to a partition"):
+            nc.sync.dma_start(out=q_loaded[:], in_=gate2[0].rearrange("(f m) -> m f", m=C2))
+        nc.scalar.activation(q_cols[:], q_loaded[:], COPY)
+        load_w2_words(1, 3)
         load_w2_scales(4, E2)
         nc.sync.dma_start(list1[:], offs)
-        load_scale_rows(nc, w1_s, w1t_scales[:, 0].rearrange("e (q r) k -> r q e k", r=4))
+        w1_rows = w1t_scales[:, 0].rearrange("e (q r) k -> r q e k", r=4)
+        for r in range(4):
+            nc.sync.dma_start(out=w1_s[r:P:32].bitcast(I32), in_=w1_rows[r].bitcast(I32))
         make_identity(nc, identity[:])
 
         slot_w, slot_s = {}, {}
@@ -104,125 +101,120 @@ def tile_moe_seb_none_kernel(
             for f in range(first // C2, last // C2):
                 by_expert[f] = tile[:, f * C2 - first : (f + 1) * C2 - first]
 
-        sums = [held.tile([P, HP, (f1 - f0) * C2], F32, name=f"sums{f0}", tag=f"sums{f0}", align_bytes=64) for f0, f1 in GROUPS]
+        sums = [
+            held.tile([P, PACK, (f1 - f0) * C2], F32, name=f"sums{f0}", tag=f"sums{f0}", align_bytes=64)
+            for f0, f1 in GROUPS
+        ]
 
-        def multiply_w2(f, s, acc):
-            cols = slice(s * P, (s + 1) * P)
+        def multiply_w2(f):
+            acc = psum.tile([P, H], F32, name="acc2", tag=f"bank{(0, 2, 0, 1, 0, 1)[f]}")
             nc.tensor.matmul_mx(
-                out=acc,
-                lhsT=w2_w[f][:, cols].bitcast(FP8X4),
-                lhsT_scale=w2_s[f // 4][4 * (f % 4) :, cols],
-                rhs=slot_w[f].bitcast(FP8X4),
-                rhs_scale=slot_s[f],
+                out=acc[:],
+                lhsT=slot_w[f].bitcast(FP8X4),
+                lhsT_scale=slot_s[f],
+                rhs=w2_w[f].bitcast(FP8X4),
+                rhs_scale=w2_s[f // 4][4 * (f % 4) :, :],
                 start=True,
                 stop=True,
             )
+            return acc[:].rearrange("m (p t) -> m t p", t=PACK)
 
-        for s in range(HP):
-            acc = psum.tile([P, C2], F32, name=f"first{s}", tag=f"bank{s}")
-            multiply_w2(0, s, acc[:])
-            nc.scalar.activation(sums[0][:, s, :], acc[:], COPY)
+        by_plane = multiply_w2(0)
+        for t0, t1 in ((0, 1), (1, PACK)):
+            rows = held.tile([P, t1 - t0, P], F32, name=f"first_rows{t0}")
+            nc.scalar.activation(rows[:], by_plane[:, t0:t1, :], COPY, scale=q_cols[:, 0:1])
+            turned = psum.tile([P, t1 - t0, C2], F32, name="first_turned", tag=f"bank{2 + t0}")
+            for t in range(t1 - t0):
+                nc.tensor.transpose(turned[:, t, :], rows[:, t, :], identity[:])
+            nc.scalar.activation(sums[0][:, t0:t1, :], turned[:], COPY)
         for c, (f0, f1) in list(enumerate(GROUPS))[1:]:
-            if c == 2:
-                load_w2_words(f0, f1)
             for f in range(f0, f1):
-                acc = psum.tile([P, HP, C2], F32, name="acc2", tag=f"bank{4 + f % 4}")
-                for s in range(HP):
-                    multiply_w2(f, s, acc[:, s, :])
-                nc.scalar.activation(sums[c][:, :, (f - f0) * C2 : (f - f0 + 1) * C2], acc[:], COPY)
+                if f == 3:
+                    load_w2_words(3, E2)
+                by_plane = multiply_w2(f)
+                rows = held.tile([P, PACK, P], F32, name="rows", tag="rows", bufs=2)
+                nc.scalar.activation(rows[:], by_plane, COPY, scale=q_cols[:, f : f + 1])
+                turned = psum.tile([P, PACK, C2], F32, name="turned", tag=f"bank{6 + f % 2}")
+                for t in range(PACK):
+                    nc.tensor.transpose(turned[:, t, :], rows[:, t, :], identity[:])
+                nc.scalar.activation(sums[c][:, :, (f - f0) * C2 : (f - f0 + 1) * C2], turned[:], COPY)
 
         w1_w = held.tile([P, E1, 2 * K], U8, name="w1_w", tag="weights", bufs=2, align_bytes=64)
         nc.sync.dma_start(out=w1_w[:].bitcast(I32), in_=w1t_words[:, 0].rearrange("e p c -> p e c").bitcast(I32))
-        g_cols = held.tile([P, BLOCKS], F32, name="g_cols", tag="slot_s0", align_bytes=64)
-        with nc.allow_non_contiguous_dma(reason="one gate value to a partition"):
-            nc.sync.dma_start(out=g_cols[:], in_=gate1[0].rearrange("(b p) -> p b", p=P))
+        g_rows = held.tile([P, T], F32, name="g_rows", tag="slot_s0", align_bytes=64)
+        nc.sync.dma_start(out=g_rows[:], in_=gate1)
 
-        dc = [held.tile([P, T], F32, name=f"dc{s}") for s in range(HP)]
+        dc = [held.tile([P, T], F32, name=f"dc{t}") for t in range(PACK)]
 
-        def scatter_dc(c, s):
+        def scatter_dc(c, t):
             first, last = GROUPS[c][0] * C2, GROUPS[c][1] * C2
+            nc.vector.tensor_copy(dc[t][:].indirect(entries(list2, first, last)), sums[c][:, t, :])
+
+        da, da_words, results = {}, {}, {}
+
+        def da_tile(e, tag):
+            da[e] = held.tile([P, PACK, C1], F32, name=f"da{e}", tag=tag, align_bytes=64)
+
+        def gather_dc(e, t):
+            first, last = e * C1, (e + 1) * C1
             nc.vector.tensor_tensor(
-                dc[s][:].indirect(entries(list2, first, last)), sums[c][:, s, :], q_rows[c][:], MULT
+                da[e][:, t, :], dc[t][:].indirect(entries(list1, first, last)), g_rows[:, first:last], MULT
             )
 
-        picked = {}
+        def round_da(e):
+            da_words[e] = held.tile([P, C1, PACK], BF16, name=f"da_words{e}", align_bytes=64)
+            nc.scalar.activation(da_words[e][:], da[e][:].rearrange("p t j -> p j t"), COPY)
 
-        def gather_dc(b0, b1, planes, tag=None):
-            name = f"picked{b0}_{planes[0]}"
-            tile = held.tile([P, len(planes), (b1 - b0) * P], F32, name=name, tag=tag or name, align_bytes=64)
-            for place, s in enumerate(planes):
-                nc.vector.tensor_copy(tile[:, place, :], dc[s][:].indirect(entries(list1, b0 * P, b1 * P)))
-                for b in range(b0, b1):
-                    picked[b, s] = tile[:, place, (b - b0) * P : (b - b0 + 1) * P]
-
-        da_words, codes, code_s, results = {}, {}, {}, {}
-
-        def weigh_and_turn(b):
-            turned = psum.tile([P, HP, P], F32, name="turned", tag=f"bank{(0, 0, 1, 2, 3, 4)[b]}")
-            for s in range(HP):
-                nc.tensor.transpose(turned[:, s, :], picked[b, s], identity[:])
-            da_rows = held.tile([P, 2, P, 2], BF16, name=f"da_rows{b}", tag=f"rows{b}", align_bytes=64)
-            nc.scalar.activation(
-                da_rows[:],
-                turned[:].rearrange("j s q -> j (s q)").rearrange("j (p u e) -> j u p e", u=2, e=2),
-                COPY,
-                scale=g_cols[:, b : b + 1],
+        def multiply_w1(e, tag):
+            codes = held.tile([P, C1], U32, name=f"codes{e}", align_bytes=64)
+            code_s = held.tile([P, C1], U8, name=f"code_s{e}", align_bytes=64)
+            nc.vector.quantize_mx(
+                out=codes[:].bitcast(FP8X4), scales=code_s[:], in_=da_words[e][:].rearrange("p j t -> p (j t)")
             )
-            back = psum.tile([P, 2, P], F32, name="back", tag=f"bank{(1, 2, 3, 4, 5, 6)[b]}")
-            pairs = da_rows[:].rearrange("j u p e -> j u (p e)").bitcast(F32)
-            for u in range(2):
-                nc.tensor.transpose(back[:, u, :], pairs[:, u, :], identity[:])
-            da_words[b] = held.tile([P, 4 * P], BF16, name=f"da_words{b}", tag=f"da_words{b}", align_bytes=64)
-            nc.scalar.copy(
-                da_words[b][:].bitcast(F32).rearrange("p (j u) -> p j u", u=2),
-                back[:].rearrange("p u j -> p j u"),
-            )
-
-        def quantise_and_multiply(b):
-            codes[b] = held.tile([P, P], U32, name=f"codes{b}", align_bytes=64)
-            code_s[b] = held.tile([P, P], U8, name=f"code_s{b}", align_bytes=64)
-            nc.vector.quantize_mx(out=codes[b][:].bitcast(FP8X4), scales=code_s[b][:], in_=da_words[b][:])
-            e = b * P // C1
-            acc = psum.tile([P, KP, P], F32, name="acc1", tag=f"bank{(0, 1, 2, 3, 4, 7)[b]}")
+            acc = psum.tile([P, KP, C1], F32, name="acc1", tag=f"bank{e}")
             for h in range(KP):
                 nc.tensor.matmul_mx(
                     out=acc[:, h, :],
                     lhsT=w1_w[:, e, 2 * P * h : 2 * P * (h + 1)].bitcast(FP4X4),
                     lhsT_scale=w1_s[:, e, h * P : (h + 1) * P],
-                    rhs=codes[b][:].bitcast(FP8X4),
-                    rhs_scale=code_s[b][:],
+                    rhs=codes[:].bitcast(FP8X4),
+                    rhs_scale=code_s[:],
                     start=True,
                     stop=True,
                 )
-            results[b] = held.tile([P, KP, P], F32, name=f"results{b}", align_bytes=64)
-            nc.scalar.activation(results[b][:], acc[:], COPY)
+            results[e] = held.tile([P, KP, C1], F32, name=f"results{e}", tag=tag, align_bytes=64)
+            nc.scalar.activation(results[e][:], acc[:], COPY)
 
         dx = [held.tile([P, T], F32, name=f"dx{h}") for h in range(KP)]
 
-        def scatter_dx(b):
+        def scatter_dx(e):
             for h in range(KP):
-                nc.vector.tensor_copy(dx[h][:].indirect(entries(list1, b * P, (b + 1) * P)), results[b][:, h, :])
+                nc.vector.tensor_copy(dx[h][:].indirect(entries(list1, e * C1, (e + 1) * C1)), results[e][:, h, :])
 
-        for c in range(2):
-            for s in range(HP):
-                scatter_dc(c, s)
-        scatter_dc(2, 0)
-        for s in range(1, HP):
-            scatter_dc(2, s)
-            gather_dc(0, 1, [s - 1])
-        gather_dc(0, 1, [HP - 1])
-        weigh_and_turn(0)
-        gather_dc(1, 2, range(HP), "q_rows3")
-        weigh_and_turn(1)
-        gather_dc(2, 4, range(HP), "sums3")
-        quantise_and_multiply(0)
-        gather_dc(4, 6, range(HP), "q_rows3")
-        for b in range(1, BLOCKS):
-            if b + 1 < BLOCKS:
-                weigh_and_turn(b + 1)
-            quantise_and_multiply(b)
-            scatter_dx(b - 1)
-        scatter_dx(BLOCKS - 1)
+        for c in range(3):
+            for t in range(PACK):
+                scatter_dc(c, t)
+        da_tile(0, "da0")
+        scatter_dc(3, 0)
+        for t in range(1, PACK):
+            scatter_dc(3, t)
+            gather_dc(0, t - 1)
+        gather_dc(0, PACK - 1)
+        round_da(0)
+        da_tile(1, "sums4")
+        for t in range(PACK):
+            gather_dc(1, t)
+        round_da(1)
+        multiply_w1(0, "sums4")
+        da_tile(2, "da0")
+        for t in range(PACK):
+            gather_dc(2, t)
+        round_da(2)
+        multiply_w1(1, "da0")
+        scatter_dx(0)
+        multiply_w1(2, "results2")
+        scatter_dx(1)
+        scatter_dx(2)
 
         for h in range(KP):
             nc.sync.dma_start(out=out[h * P : (h + 1) * P, :], in_=dx[h][:])

@@ -40,8 +40,8 @@ def tile_moe_seb_none_kernel(
 
         list2 = held.tile([P, T // LIST], U16, name="list2")
         list1 = held.tile([P, T // LIST], U16, name="list1")
-        dy_w = held.tile([P, WINDOW], U32, name="dy_w", align_bytes=64)
-        dy_s = held.tile([P, WINDOW], U8, name="dy_s", align_bytes=64)
+        dy_w = held.tile([P, WINDOW], U32, name="dy_w", tag="dy_w", align_bytes=64)
+        dy_s = held.tile([P, T], U8, name="dy_s", align_bytes=64)
         w2_s = [held.tile([P, H], U8, name=f"w2_s{a}", align_bytes=64) for a in range(2)]
         w1_s = held.tile([P, E1, K], U8, name="w1_s", align_bytes=64)
         q_loaded = held.tile([P, E2], F32, name="q_loaded")
@@ -49,7 +49,6 @@ def tile_moe_seb_none_kernel(
         identity = held.tile([P, P], F32, name="identity")
 
         nc.vector.memset(w2_s[0][:].bitcast(I32), 0)
-        nc.vector.memset(dy_s[:, T:].bitcast(I32), 0)
         nc.vector.memset(dy_w[:, T:].bitcast(I32), 0)
         nc.vector.memset(w2_s[1][:].bitcast(I32), 0)
         nc.vector.memset(w1_s[:].bitcast(I32), 0)
@@ -74,15 +73,15 @@ def tile_moe_seb_none_kernel(
         for q in range(4):
             rows = dy_scales[0, 4 * q : 4 * q + 4, :].bitcast(I32)
             (nc.sync, nc.scalar)[q // 2].dma_start(
-                out=dy_s[32 * q : 32 * q + 32, :T].bitcast(I32), in_=rows.unsqueeze(0).to_broadcast([8, 4, T // 4])
+                out=dy_s[32 * q : 32 * q + 32, :].bitcast(I32), in_=rows.unsqueeze(0).to_broadcast([8, 4, T // 4])
             )
         nc.sync.dma_start(out=dy_w[:, :T].bitcast(I32), in_=dy_words[0].rearrange("p t d -> p (t d)").bitcast(I32))
-        load_w2_words(*GROUPS[0])
+        load_w2_words(0, 2)
         load_w2_scales(0, 4)
         with nc.allow_non_contiguous_dma(reason="one gate value to a partition"):
             nc.sync.dma_start(out=q_loaded[:], in_=gate2[0].rearrange("(f m) -> m f", m=C2))
         nc.scalar.activation(q_cols[:], q_loaded[:], COPY)
-        load_w2_words(1, 3)
+        load_w2_words(2, 4)
         load_w2_scales(4, E2)
         nc.sync.dma_start(list1[:], offs)
         w1_rows = w1t_scales[:, 0].rearrange("e (q r) k -> r q e k", r=4)
@@ -91,12 +90,13 @@ def tile_moe_seb_none_kernel(
         make_identity(nc, identity[:])
 
         slot_w, slot_s = {}, {}
-        for table, dtype, by_expert, name, first, last in (
-            (dy_s, U8, slot_s, "slot_s", 0, T),
-            (dy_w, U32, slot_w, "slot_w", 0, C2),
-            (dy_w, U32, slot_w, "slot_w", C2, T),
+        for table, dtype, by_expert, first, last, tag in (
+            (dy_s, U8, slot_s, 0, T // 2, "slot_s0"),
+            (dy_w, U32, slot_w, 0, C2, "slot_w0"),
+            (dy_w, U32, slot_w, C2, T, "slot_w1"),
+            (dy_s, U8, slot_s, T // 2, T, "dy_w"),
         ):
-            tile = held.tile([P, last - first], dtype, name=f"{name}{first}", tag=f"{name}{first}", align_bytes=64)
+            tile = held.tile([P, last - first], dtype, name=f"slots{first}", tag=tag, align_bytes=64)
             nc.vector.tensor_copy(tile[:], table[:].indirect(entries(list2, first, last)))
             for f in range(first // C2, last // C2):
                 by_expert[f] = tile[:, f * C2 - first : (f + 1) * C2 - first]
@@ -107,7 +107,7 @@ def tile_moe_seb_none_kernel(
         ]
 
         def multiply_w2(f):
-            acc = psum.tile([P, H], F32, name="acc2", tag=f"bank{(0, 2, 0, 1, 0, 1)[f]}")
+            acc = psum.tile([P, H], F32, name="acc2", tag=f"bank{(0, 2, 3, 2, 3, 2)[f]}")
             nc.tensor.matmul_mx(
                 out=acc[:],
                 lhsT=slot_w[f].bitcast(FP8X4),
@@ -119,25 +119,25 @@ def tile_moe_seb_none_kernel(
             )
             return acc[:].rearrange("m (p t) -> m t p", t=PACK)
 
-        by_plane = multiply_w2(0)
-        for t0, t1 in ((0, 1), (1, PACK)):
-            rows = held.tile([P, t1 - t0, P], F32, name=f"first_rows{t0}")
-            nc.scalar.activation(rows[:], by_plane[:, t0:t1, :], COPY, scale=q_cols[:, 0:1])
-            turned = psum.tile([P, t1 - t0, C2], F32, name="first_turned", tag=f"bank{2 + t0}")
+        def weigh_and_turn(f, by_plane, t0, t1, bank):
+            c = [f0 <= f < f1 for f0, f1 in GROUPS].index(True)
+            rows = held.tile([P, t1 - t0, P], F32, name=f"rows{f}_{t0}")
+            nc.scalar.activation(rows[:], by_plane[:, t0:t1, :], COPY, scale=q_cols[:, f : f + 1])
+            turned = psum.tile([P, t1 - t0, C2], F32, name="turned", tag=f"bank{bank}")
             for t in range(t1 - t0):
                 nc.tensor.transpose(turned[:, t, :], rows[:, t, :], identity[:])
-            nc.scalar.activation(sums[0][:, t0:t1, :], turned[:], COPY)
-        for c, (f0, f1) in list(enumerate(GROUPS))[1:]:
-            for f in range(f0, f1):
-                if f == 3:
-                    load_w2_words(3, E2)
-                by_plane = multiply_w2(f)
-                rows = held.tile([P, PACK, P], F32, name="rows", tag="rows", bufs=2)
-                nc.scalar.activation(rows[:], by_plane, COPY, scale=q_cols[:, f : f + 1])
-                turned = psum.tile([P, PACK, C2], F32, name="turned", tag=f"bank{6 + f % 2}")
-                for t in range(PACK):
-                    nc.tensor.transpose(turned[:, t, :], rows[:, t, :], identity[:])
-                nc.scalar.activation(sums[c][:, :, (f - f0) * C2 : (f - f0 + 1) * C2], turned[:], COPY)
+            place = (f - GROUPS[c][0]) * C2
+            nc.scalar.activation(sums[c][:, t0:t1, place : place + C2], turned[:], COPY)
+
+        for f in range(E2):
+            if f == 4:
+                load_w2_words(4, E2)
+            by_plane = multiply_w2(f)
+            if f < 2:
+                weigh_and_turn(f, by_plane, 0, 1, 2 + 2 * f)
+                weigh_and_turn(f, by_plane, 1, PACK, 3 + 2 * f)
+            else:
+                weigh_and_turn(f, by_plane, 0, PACK, 6 + f % 2)
 
         w1_w = held.tile([P, E1, 2 * K], U8, name="w1_w", tag="weights", bufs=2, align_bytes=64)
         nc.sync.dma_start(out=w1_w[:].bitcast(I32), in_=w1t_words[:, 0].rearrange("e p c -> p e c").bitcast(I32))

@@ -44,8 +44,7 @@ def tile_moe_seb_none_kernel(
         dy_s = held.tile([P, T], U8, name="dy_s", align_bytes=64)
         w2_s = [held.tile([P, H], U8, name=f"w2_s{a}", align_bytes=64) for a in range(2)]
         w1_s = held.tile([P, E1, K], U8, name="w1_s", align_bytes=64)
-        q_loaded = held.tile([P, E2], F32, name="q_loaded")
-        q_cols = held.tile([P, E2], F32, name="q_cols")
+        q_rows = [held.tile([P, (f1 - f0) * C2], F32, name=f"q_rows{f0}") for f0, f1 in GROUPS]
         identity = held.tile([P, P], F32, name="identity")
 
         nc.vector.memset(w2_s[0][:].bitcast(I32), 0)
@@ -59,6 +58,9 @@ def tile_moe_seb_none_kernel(
                     out=w2_s[f0 // 4][32 * q : 32 * q + 4 * (f1 - f0), :].bitcast(I32),
                     in_=w2t_scales[f0:f1, 0, 4 * q : 4 * q + 4, :].bitcast(I32),
                 )
+
+        def load_q_rows(c):
+            nc.sync.dma_start(out=q_rows[c][:], in_=gate2[:, GROUPS[c][0] * C2 : GROUPS[c][1] * C2])
 
         w2_w = {}
 
@@ -76,13 +78,14 @@ def tile_moe_seb_none_kernel(
                 out=dy_s[32 * q : 32 * q + 32, :].bitcast(I32), in_=rows.unsqueeze(0).to_broadcast([8, 4, T // 4])
             )
         nc.sync.dma_start(out=dy_w[:, :T].bitcast(I32), in_=dy_words[0].rearrange("p t d -> p (t d)").bitcast(I32))
-        load_w2_words(0, 2)
+        load_w2_words(0, 1)
         load_w2_scales(0, 4)
-        with nc.allow_non_contiguous_dma(reason="one gate value to a partition"):
-            nc.sync.dma_start(out=q_loaded[:], in_=gate2[0].rearrange("(f m) -> m f", m=C2))
-        nc.scalar.activation(q_cols[:], q_loaded[:], COPY)
-        load_w2_words(2, 4)
+        load_q_rows(0)
+        load_w2_words(1, 3)
+        load_q_rows(1)
+        load_q_rows(2)
         load_w2_scales(4, E2)
+        load_q_rows(3)
         nc.sync.dma_start(list1[:], offs)
         w1_rows = w1t_scales[:, 0].rearrange("e (q r) k -> r q e k", r=4)
         for r in range(4):
@@ -122,7 +125,7 @@ def tile_moe_seb_none_kernel(
         def weigh_and_turn(f, by_plane, t0, t1, bank):
             c = [f0 <= f < f1 for f0, f1 in GROUPS].index(True)
             rows = held.tile([P, t1 - t0, P], F32, name=f"rows{f}_{t0}")
-            nc.scalar.activation(rows[:], by_plane[:, t0:t1, :], COPY, scale=q_cols[:, f : f + 1])
+            nc.scalar.activation(rows[:], by_plane[:, t0:t1, :], COPY)
             turned = psum.tile([P, t1 - t0, C2], F32, name="turned", tag=f"bank{bank}")
             for t in range(t1 - t0):
                 nc.tensor.transpose(turned[:, t, :], rows[:, t, :], identity[:])
@@ -130,8 +133,8 @@ def tile_moe_seb_none_kernel(
             nc.scalar.activation(sums[c][:, t0:t1, place : place + C2], turned[:], COPY)
 
         for f in range(E2):
-            if f == 4:
-                load_w2_words(4, E2)
+            if f == 3:
+                load_w2_words(3, E2)
             by_plane = multiply_w2(f)
             if f < 2:
                 weigh_and_turn(f, by_plane, 0, 1, 2 + 2 * f)
@@ -148,7 +151,9 @@ def tile_moe_seb_none_kernel(
 
         def scatter_dc(c, t):
             first, last = GROUPS[c][0] * C2, GROUPS[c][1] * C2
-            nc.vector.tensor_copy(dc[t][:].indirect(entries(list2, first, last)), sums[c][:, t, :])
+            nc.vector.tensor_tensor(
+                dc[t][:].indirect(entries(list2, first, last)), sums[c][:, t, :], q_rows[c][:], MULT
+            )
 
         da, da_words, results = {}, {}, {}
 

@@ -94,10 +94,10 @@ def tile_moe_seb_none_kernel(
 
         slot_w, slot_s = {}, {}
         for table, dtype, by_expert, first, last, tag in (
-            (dy_s, U8, slot_s, 0, T // 2, "slot_s0"),
+            (dy_s, U8, slot_s, 0, 4 * C2, "slot_s0"),
             (dy_w, U32, slot_w, 0, C2, "slot_w0"),
             (dy_w, U32, slot_w, C2, T, "slot_w1"),
-            (dy_s, U8, slot_s, T // 2, T, "dy_w"),
+            (dy_s, U8, slot_s, 4 * C2, T, "dy_w"),
         ):
             tile = held.tile([P, last - first], dtype, name=f"slots{first}", tag=tag, align_bytes=64)
             nc.vector.tensor_copy(tile[:], table[:].indirect(entries(list2, first, last)))
@@ -110,7 +110,7 @@ def tile_moe_seb_none_kernel(
         ]
 
         def multiply_w2(f):
-            acc = psum.tile([P, H], F32, name="acc2", tag=f"bank{(0, 2, 3, 2, 3, 2)[f]}")
+            acc = psum.tile([P, H], F32, name="acc2", tag=f"bank{(0, 1, 2, 1, 2, 1)[f]}")
             nc.tensor.matmul_mx(
                 out=acc[:],
                 lhsT=slot_w[f].bitcast(FP8X4),
@@ -122,25 +122,46 @@ def tile_moe_seb_none_kernel(
             )
             return acc[:].rearrange("m (p t) -> m t p", t=PACK)
 
-        def weigh_and_turn(f, by_plane, t0, t1, bank):
+        def turn_planes(f, by_plane, t0, t1, banks):
             c = [f0 <= f < f1 for f0, f1 in GROUPS].index(True)
-            rows = held.tile([P, t1 - t0, P], F32, name=f"rows{f}_{t0}")
-            nc.scalar.activation(rows[:], by_plane[:, t0:t1, :], COPY)
-            turned = psum.tile([P, t1 - t0, C2], F32, name="turned", tag=f"bank{bank}")
-            for t in range(t1 - t0):
-                nc.tensor.transpose(turned[:, t, :], rows[:, t, :], identity[:])
             place = (f - GROUPS[c][0]) * C2
-            nc.scalar.activation(sums[c][:, t0:t1, place : place + C2], turned[:], COPY)
+            rows = held.tile([P, PACK, P], F32, name=f"rows{f}_{t0}")
+            nc.scalar.activation(rows[:, t0:t1, :], by_plane[:, t0:t1, :], COPY)
+            for bank, (u0, u1) in banks.items():
+                turned = psum.tile([P, u1 - u0, C2], F32, name="turned", tag=f"bank{bank}")
+                for t in range(u0, u1):
+                    nc.tensor.transpose(turned[:, t - u0, :], rows[:, t, :], identity[:])
+                nc.scalar.activation(sums[c][:, u0:u1, place : place + C2], turned[:], COPY)
+
+        def first_planes(banks):
+            words = held.tile([P, len(banks), P], U32, name="plane_w", align_bytes=64)
+            nc.gpsimd.tensor_copy(words[:], w2_w[0].rearrange("p (m t) -> p t m", t=PACK)[:, : len(banks), :])
+            for t, bank in enumerate(banks):
+                scales = held.tile([P, P], U8, name=f"plane_s{t}", align_bytes=64)
+                nc.gpsimd.tensor_copy(scales[:], w2_s[0][:, t:H:PACK])
+                acc = psum.tile([P, C2], F32, name="plane", tag=f"bank{bank}")
+                nc.tensor.matmul_mx(
+                    out=acc[:],
+                    lhsT=words[:, t, :].bitcast(FP8X4),
+                    lhsT_scale=scales[:],
+                    rhs=slot_w[0].bitcast(FP8X4),
+                    rhs_scale=slot_s[0],
+                    start=True,
+                    stop=True,
+                )
+                nc.scalar.activation(sums[0][:, t, :], acc[:], COPY)
 
         for f in range(E2):
             if f == 3:
                 load_w2_words(3, E2)
             by_plane = multiply_w2(f)
-            if f < 2:
-                weigh_and_turn(f, by_plane, 0, 1, 2 + 2 * f)
-                weigh_and_turn(f, by_plane, 1, PACK, 3 + 2 * f)
+            if f == 0:
+                first_planes((1, 2))
+                turn_planes(f, by_plane, 2, PACK, {3: (2, PACK)})
+            elif f == 1:
+                turn_planes(f, by_plane, 0, PACK, {2 + 2 * f: (0, 1), 3 + 2 * f: (1, PACK)})
             else:
-                weigh_and_turn(f, by_plane, 0, PACK, 6 + f % 2)
+                turn_planes(f, by_plane, 0, PACK, {6 + f % 2: (0, PACK)})
 
         w1_w = held.tile([P, E1, 2 * K], U8, name="w1_w", tag="weights", bufs=2, align_bytes=64)
         nc.sync.dma_start(out=w1_w[:].bitcast(I32), in_=w1t_words[:, 0].rearrange("e p c -> p e c").bitcast(I32))

@@ -22,7 +22,7 @@ P = 128
 LIST = 16
 PACK = 4
 KP = K // P
-GROUPS = ((0, 1), (1, 2), (2, 4), (4, 6))
+GROUPS = ((0, 1), (1, 2), (2, 3), (3, 6))
 WINDOW = 1024
 
 
@@ -48,7 +48,6 @@ def tile_moe_seb_none_kernel(
         identity = held.tile([P, P], F32, name="identity")
 
         nc.vector.memset(w2_s[0][:].bitcast(I32), 0)
-        nc.vector.memset(dy_w[:, T:].bitcast(I32), 0)
         nc.vector.memset(w2_s[1][:].bitcast(I32), 0)
         nc.vector.memset(w1_s[:].bitcast(I32), 0)
 
@@ -64,8 +63,8 @@ def tile_moe_seb_none_kernel(
 
         w2_w = {}
 
-        def load_w2_words(f0, f1):
-            tile = held.tile([P, f1 - f0, H], U32, name=f"w2_w{f0}", tag="weights", bufs=2, align_bytes=64)
+        def load_w2_words(f0, f1, tag="weights", bufs=2):
+            tile = held.tile([P, f1 - f0, H], U32, name=f"w2_w{f0}", tag=tag, bufs=bufs, align_bytes=64)
             src = w2t_words[f0:f1, 0].rearrange("f p i d -> p f (i d)")
             nc.sync.dma_start(out=tile[:].bitcast(I32), in_=src.bitcast(I32))
             for f in range(f0, f1):
@@ -83,6 +82,7 @@ def tile_moe_seb_none_kernel(
         load_q_rows(0)
         load_w2_words(1, 3)
         load_q_rows(1)
+        load_w2_words(3, 4, "w2_w3", 1)
         load_q_rows(2)
         load_w2_scales(4, E2)
         load_q_rows(3)
@@ -110,7 +110,7 @@ def tile_moe_seb_none_kernel(
         ]
 
         def multiply_w2(f):
-            acc = psum.tile([P, H], F32, name="acc2", tag=f"bank{(0, 1, 2, 1, 2, 1)[f]}")
+            acc = psum.tile([P, H], F32, name="acc2", tag=f"bank{(0, 0, 0, 4, 0, 4)[f]}")
             nc.tensor.matmul_mx(
                 out=acc[:],
                 lhsT=slot_w[f].bitcast(FP8X4),
@@ -152,8 +152,8 @@ def tile_moe_seb_none_kernel(
                 nc.scalar.activation(sums[0][:, t, :], acc[:], COPY)
 
         for f in range(E2):
-            if f == 3:
-                load_w2_words(3, E2)
+            if f == 4:
+                load_w2_words(4, E2)
             by_plane = multiply_w2(f)
             if f == 0:
                 first_planes((1, 2))
@@ -217,21 +217,18 @@ def tile_moe_seb_none_kernel(
             for h in range(KP):
                 nc.vector.tensor_copy(dx[h][:].indirect(entries(list1, e * C1, (e + 1) * C1)), results[e][:, h, :])
 
-        for c in range(3):
+        for c in range(len(GROUPS)):
             for t in range(PACK):
                 scatter_dc(c, t)
         da_tile(0, "da0")
-        scatter_dc(3, 0)
-        for t in range(1, PACK):
-            scatter_dc(3, t)
-            gather_dc(0, t - 1)
-        gather_dc(0, PACK - 1)
+        for t in range(PACK):
+            gather_dc(0, t)
         round_da(0)
-        da_tile(1, "sums4")
+        da_tile(1, "sums3")
         for t in range(PACK):
             gather_dc(1, t)
         round_da(1)
-        multiply_w1(0, "sums4")
+        multiply_w1(0, "sums3")
         da_tile(2, "da0")
         for t in range(PACK):
             gather_dc(2, t)

@@ -109,8 +109,8 @@ def tile_moe_seb_none_kernel(
             for f0, f1 in GROUPS
         ]
 
-        def multiply_w2(f):
-            acc = psum.tile([P, H], F32, name="acc2", tag=f"bank{(0, 0, 0, 4, 0, 4)[f]}")
+        def multiply_w2(f, bank):
+            acc = psum.tile([P, H], F32, name="acc2", tag=f"bank{bank}")
             nc.tensor.matmul_mx(
                 out=acc[:],
                 lhsT=slot_w[f].bitcast(FP8X4),
@@ -151,17 +151,17 @@ def tile_moe_seb_none_kernel(
                 )
                 nc.scalar.activation(sums[0][:, t, :], acc[:], COPY)
 
-        for f in range(E2):
-            if f == 4:
+        for step, f in enumerate((0, 1, 2, 3, 5, 4)):
+            if step == 4:
                 load_w2_words(4, E2)
-            by_plane = multiply_w2(f)
+            by_plane = multiply_w2(f, (0, 0, 0, 4, 0, 4)[step])
             if f == 0:
                 first_planes((1, 2))
                 turn_planes(f, by_plane, 2, PACK, {3: (2, PACK)})
             elif f == 1:
                 turn_planes(f, by_plane, 0, PACK, {2 + 2 * f: (0, 1), 3 + 2 * f: (1, PACK)})
             else:
-                turn_planes(f, by_plane, 0, PACK, {6 + f % 2: (0, PACK)})
+                turn_planes(f, by_plane, 0, PACK, {6 + step % 2: (0, PACK)})
 
         w1_w = held.tile([P, E1, 2 * K], U8, name="w1_w", tag="weights", bufs=2, align_bytes=64)
         nc.sync.dma_start(out=w1_w[:].bitcast(I32), in_=w1t_words[:, 0].rearrange("e p c -> p e c").bitcast(I32))
@@ -170,10 +170,12 @@ def tile_moe_seb_none_kernel(
 
         dc = [held.tile([P, T], F32, name=f"dc{t}") for t in range(PACK)]
 
-        def scatter_dc(c, t):
-            first, last = GROUPS[c][0] * C2, GROUPS[c][1] * C2
+        def scatter_dc(c, t, part=0, parts=1):
+            width = (GROUPS[c][1] - GROUPS[c][0]) * C2 // parts
+            cols = slice(part * width, (part + 1) * width)
+            first = GROUPS[c][0] * C2 + part * width
             nc.vector.tensor_tensor(
-                dc[t][:].indirect(entries(list2, first, last)), sums[c][:, t, :], q_rows[c][:], MULT
+                dc[t][:].indirect(entries(list2, first, first + width)), sums[c][:, t, cols], q_rows[c][:, cols], MULT
             )
 
         da, da_words, results = {}, {}, {}
@@ -181,10 +183,14 @@ def tile_moe_seb_none_kernel(
         def da_tile(e, tag):
             da[e] = held.tile([P, PACK, C1], F32, name=f"da{e}", tag=tag, align_bytes=64)
 
-        def gather_dc(e, t):
-            first, last = e * C1, (e + 1) * C1
+        def gather_dc(e, t, part=0, parts=1):
+            width = C1 // parts
+            first = e * C1 + part * width
             nc.vector.tensor_tensor(
-                da[e][:, t, :], dc[t][:].indirect(entries(list1, first, last)), g_rows[:, first:last], MULT
+                da[e][:, t, part * width : (part + 1) * width],
+                dc[t][:].indirect(entries(list1, first, first + width)),
+                g_rows[:, first : first + width],
+                MULT,
             )
 
         def round_da(e):
@@ -217,11 +223,17 @@ def tile_moe_seb_none_kernel(
             for h in range(KP):
                 nc.vector.tensor_copy(dx[h][:].indirect(entries(list1, e * C1, (e + 1) * C1)), results[e][:, h, :])
 
-        for c in range(len(GROUPS)):
+        for c in range(3):
             for t in range(PACK):
                 scatter_dc(c, t)
         da_tile(0, "da0")
-        for t in range(PACK):
+        for t in range(2):
+            scatter_dc(3, t)
+        for t in range(2):
+            for part in range(2):
+                gather_dc(0, t, part, 2)
+                scatter_dc(3, 2 + part, t, 2)
+        for t in range(2, PACK):
             gather_dc(0, t)
         round_da(0)
         da_tile(1, "sums3")

@@ -22,8 +22,10 @@ P = 128
 LIST = 16
 PACK = 4
 KP = K // P
-GROUPS = ((0, 1), (1, 2), (2, 3), (3, 6))
+GROUPS = ((0, 1), (1, 2), (2, 3), (3, 4), (4, 5), (5, 6))
+UNITS = ((0, 128), (128, 256), (256, 512), (512, 768))
 WINDOW = 1024
+PIECE = 256
 
 
 def entries(offsets, first, last):
@@ -36,6 +38,7 @@ def tile_moe_seb_none_kernel(
     nc = tc.nc
     with ExitStack() as ctx:
         held = ctx.enter_context(tc.tile_pool(name="held", bufs=1))
+        shared = ctx.enter_context(tc.tile_pool(name="shared", bufs=1))
         psum = ctx.enter_context(tc.psum_pool(name="psum", bufs=1))
 
         list2 = held.tile([P, T // LIST], U16, name="list2")
@@ -44,7 +47,9 @@ def tile_moe_seb_none_kernel(
         dy_s = held.tile([P, T], U8, name="dy_s", align_bytes=64)
         w2_s = [held.tile([P, H], U8, name=f"w2_s{a}", align_bytes=64) for a in range(2)]
         w1_s = held.tile([P, E1, K], U8, name="w1_s", align_bytes=64)
-        q_rows = [held.tile([P, (f1 - f0) * C2], F32, name=f"q_rows{f0}") for f0, f1 in GROUPS]
+        w1_w = held.tile([P, E1, 2 * K], U8, name="w1_w", align_bytes=64)
+        q_rows = held.tile([P, T], F32, name="q_rows")
+        g_rows = held.tile([P, T], F32, name="g_rows")
         identity = held.tile([P, P], F32, name="identity")
 
         nc.vector.memset(w2_s[0][:].bitcast(I32), 0)
@@ -58,13 +63,13 @@ def tile_moe_seb_none_kernel(
                     in_=w2t_scales[f0:f1, 0, 4 * q : 4 * q + 4, :].bitcast(I32),
                 )
 
-        def load_q_rows(c):
-            nc.sync.dma_start(out=q_rows[c][:], in_=gate2[:, GROUPS[c][0] * C2 : GROUPS[c][1] * C2])
+        def load_q_rows(f0, f1):
+            nc.sync.dma_start(out=q_rows[:, f0 * C2 : f1 * C2], in_=gate2[:, f0 * C2 : f1 * C2])
 
         w2_w = {}
 
-        def load_w2_words(f0, f1, tag="weights", bufs=2):
-            tile = held.tile([P, f1 - f0, H], U32, name=f"w2_w{f0}", tag=tag, bufs=bufs, align_bytes=64)
+        def load_w2_words(f0, f1):
+            tile = held.tile([P, f1 - f0, H], U32, name=f"w2_w{f0}", align_bytes=64)
             src = w2t_words[f0:f1, 0].rearrange("f p i d -> p f (i d)")
             nc.sync.dma_start(out=tile[:].bitcast(I32), in_=src.bitcast(I32))
             for f in range(f0, f1):
@@ -77,26 +82,27 @@ def tile_moe_seb_none_kernel(
                 out=dy_s[32 * q : 32 * q + 32, :].bitcast(I32), in_=rows.unsqueeze(0).to_broadcast([8, 4, T // 4])
             )
         nc.sync.dma_start(out=dy_w[:, :T].bitcast(I32), in_=dy_words[0].rearrange("p t d -> p (t d)").bitcast(I32))
-        load_w2_words(0, 1)
+        load_w2_words(0, 2)
         load_w2_scales(0, 4)
-        load_q_rows(0)
-        load_w2_words(1, 3)
-        load_q_rows(1)
-        load_w2_words(3, 4, "w2_w3", 1)
-        load_q_rows(2)
+        load_q_rows(0, 2)
+        load_w2_words(2, 3)
+        load_w2_words(3, E2)
         load_w2_scales(4, E2)
-        load_q_rows(3)
+        load_q_rows(2, E2)
+        nc.sync.dma_start(out=g_rows[:], in_=gate1)
         nc.sync.dma_start(list1[:], offs)
         w1_rows = w1t_scales[:, 0].rearrange("e (q r) k -> r q e k", r=4)
         for r in range(4):
             nc.sync.dma_start(out=w1_s[r:P:32].bitcast(I32), in_=w1_rows[r].bitcast(I32))
+        nc.sync.dma_start(out=w1_w[:].bitcast(I32), in_=w1t_words[:, 0].rearrange("e p c -> p e c").bitcast(I32))
         make_identity(nc, identity[:])
 
         slot_w, slot_s = {}, {}
         for table, dtype, by_expert, first, last, tag in (
             (dy_s, U8, slot_s, 0, 4 * C2, "slot_s0"),
             (dy_w, U32, slot_w, 0, C2, "slot_w0"),
-            (dy_w, U32, slot_w, C2, T, "slot_w1"),
+            (dy_w, U32, slot_w, C2, 2 * C2, "slot_w1"),
+            (dy_w, U32, slot_w, 2 * C2, T, "slot_w2"),
             (dy_s, U8, slot_s, 4 * C2, T, "dy_w"),
         ):
             tile = held.tile([P, last - first], dtype, name=f"slots{first}", tag=tag, align_bytes=64)
@@ -104,10 +110,11 @@ def tile_moe_seb_none_kernel(
             for f in range(first // C2, last // C2):
                 by_expert[f] = tile[:, f * C2 - first : (f + 1) * C2 - first]
 
-        sums = [
-            held.tile([P, PACK, (f1 - f0) * C2], F32, name=f"sums{f0}", tag=f"sums{f0}", align_bytes=64)
-            for f0, f1 in GROUPS
+        early = [
+            held.tile([P, 2, (f1 - f0) * C2], F32, name=f"early{f0}") for f0, f1 in GROUPS[:-1]
         ]
+        late = [held.tile([P, 2, PIECE], F32, name=f"late{c}") for c in range(T // PIECE)]
+        rows, products = {}, {}
 
         def multiply_w2(f, bank):
             acc = psum.tile([P, H], F32, name="acc2", tag=f"bank{bank}")
@@ -120,136 +127,174 @@ def tile_moe_seb_none_kernel(
                 start=True,
                 stop=True,
             )
-            return acc[:].rearrange("m (p t) -> m t p", t=PACK)
+            rows[f] = held.tile([P, PACK, P], F32, name=f"rows{f}")
+            products[f] = acc[:].rearrange("m (p t) -> m t p", t=PACK)
 
-        def turn_planes(f, by_plane, t0, t1, banks):
-            c = [f0 <= f < f1 for f0, f1 in GROUPS].index(True)
-            place = (f - GROUPS[c][0]) * C2
-            rows = held.tile([P, PACK, P], F32, name=f"rows{f}_{t0}")
-            nc.scalar.activation(rows[:, t0:t1, :], by_plane[:, t0:t1, :], COPY)
-            for bank, (u0, u1) in banks.items():
-                turned = psum.tile([P, u1 - u0, C2], F32, name="turned", tag=f"bank{bank}")
-                for t in range(u0, u1):
-                    nc.tensor.transpose(turned[:, t - u0, :], rows[:, t, :], identity[:])
-                nc.scalar.activation(sums[c][:, u0:u1, place : place + C2], turned[:], COPY)
+        def copy_rows(f, t0, t1):
+            nc.scalar.activation(rows[f][:, t0:t1, :], products[f][:, t0:t1, :], COPY)
+
+        def turn(experts, t0, bank, target):
+            turned = psum.tile([P, 2, len(experts) * C2], F32, name="turned", tag=f"bank{bank}")
+            for t in range(2):
+                for n, f in enumerate(experts):
+                    nc.tensor.transpose(turned[:, t, n * C2 : (n + 1) * C2], rows[f][:, t0 + t, :], identity[:])
+            nc.scalar.activation(target, turned[:], COPY)
 
         def first_planes(banks):
-            words = held.tile([P, len(banks), P], U32, name="plane_w", align_bytes=64)
-            nc.gpsimd.tensor_copy(words[:], w2_w[0].rearrange("p (m t) -> p t m", t=PACK)[:, : len(banks), :])
             for t, bank in enumerate(banks):
+                words = held.tile([P, P], U32, name=f"plane_w{t}", align_bytes=64)
+                nc.gpsimd.tensor_copy(words[:], w2_w[0][:, t:H:PACK])
                 scales = held.tile([P, P], U8, name=f"plane_s{t}", align_bytes=64)
                 nc.gpsimd.tensor_copy(scales[:], w2_s[0][:, t:H:PACK])
                 acc = psum.tile([P, C2], F32, name="plane", tag=f"bank{bank}")
                 nc.tensor.matmul_mx(
                     out=acc[:],
-                    lhsT=words[:, t, :].bitcast(FP8X4),
+                    lhsT=words[:].bitcast(FP8X4),
                     lhsT_scale=scales[:],
                     rhs=slot_w[0].bitcast(FP8X4),
                     rhs_scale=slot_s[0],
                     start=True,
                     stop=True,
                 )
-                nc.scalar.activation(sums[0][:, t, :], acc[:], COPY)
+                nc.scalar.activation(early[0][:, t, :], acc[:], COPY)
 
-        for step, f in enumerate((0, 1, 2, 3, 5, 4)):
-            if step == 4:
-                load_w2_words(4, E2)
-            by_plane = multiply_w2(f, (0, 0, 0, 4, 0, 4)[step])
-            if f == 0:
-                first_planes((1, 2))
-                turn_planes(f, by_plane, 2, PACK, {3: (2, PACK)})
-            elif f == 1:
-                turn_planes(f, by_plane, 0, PACK, {2 + 2 * f: (0, 1), 3 + 2 * f: (1, PACK)})
-            else:
-                turn_planes(f, by_plane, 0, PACK, {6 + step % 2: (0, PACK)})
+        first_planes((0, 1))
+        multiply_w2(1, 2)
+        copy_rows(1, 0, 2)
+        turn((1,), 0, 3, early[1][:])
+        multiply_w2(2, 0)
+        copy_rows(2, 0, PACK)
+        turn((2,), 0, 4, early[2][:])
+        multiply_w2(3, 1)
+        copy_rows(3, 0, PACK)
+        turn((3,), 0, 3, early[3][:])
+        multiply_w2(4, 0)
+        copy_rows(4, 0, PACK)
+        turn((4,), 0, 4, early[4][:])
+        copy_rows(1, 2, PACK)
+        multiply_w2(0, 1)
+        copy_rows(0, 2, PACK)
+        multiply_w2(5, 0)
+        copy_rows(5, 0, PACK)
+        turn((0, 1), 2, 5, late[0][:])
+        last = shared.tile([P, 2, C2], F32, name="last", offset=4 * (T - C2))
+        turn((5,), 0, 5, last[:])
+        turn((2, 3), 2, 4, late[1][:])
+        turn((4, 5), 2, 3, late[2][:])
+        early.append(last)
 
-        w1_w = held.tile([P, E1, 2 * K], U8, name="w1_w", tag="weights", bufs=2, align_bytes=64)
-        nc.sync.dma_start(out=w1_w[:].bitcast(I32), in_=w1t_words[:, 0].rearrange("e p c -> p e c").bitcast(I32))
-        g_rows = held.tile([P, T], F32, name="g_rows", tag="slot_s0", align_bytes=64)
-        nc.sync.dma_start(out=g_rows[:], in_=gate1)
+        dc = [held.tile([P, T], F32, name=f"dc{t}") for t in range(2)]
 
-        dc = [held.tile([P, T], F32, name=f"dc{t}") for t in range(PACK)]
-
-        def scatter_dc(c, t, part=0, parts=1):
-            width = (GROUPS[c][1] - GROUPS[c][0]) * C2 // parts
-            cols = slice(part * width, (part + 1) * width)
-            first = GROUPS[c][0] * C2 + part * width
+        def scatter_dc(t, sums, first, last):
             nc.vector.tensor_tensor(
-                dc[t][:].indirect(entries(list2, first, first + width)), sums[c][:, t, cols], q_rows[c][:, cols], MULT
+                dc[t][:].indirect(entries(list2, first, last)), sums, q_rows[:, first:last], MULT
             )
 
-        da, da_words, results = {}, {}, {}
+        for c, (f0, f1) in enumerate(GROUPS):
+            for t in range(2):
+                scatter_dc(t, early[c][:, t, :], f0 * C2, f1 * C2)
+        dc.extend(shared.tile([P, T], F32, name=f"dc{2 + t}", offset=4 * T * t) for t in range(2))
 
-        def da_tile(e, tag):
-            da[e] = held.tile([P, PACK, C1], F32, name=f"da{e}", tag=tag, align_bytes=64)
+        starts = (2 * C1 + C1 // 2, 6 * C1 + C1 // 2, 0)
+        da = held.tile([P, starts[1] + PACK * C1], F32, name="da", align_bytes=64)
+        planes = [da[:, s : s + PACK * C1].rearrange("p (t j) -> p t j", t=PACK) for s in starts]
 
-        def gather_dc(e, t, part=0, parts=1):
-            width = C1 // parts
-            first = e * C1 + part * width
+        def gather_dc(t, first, last):
+            e = first // C1
             nc.vector.tensor_tensor(
-                da[e][:, t, part * width : (part + 1) * width],
-                dc[t][:].indirect(entries(list1, first, first + width)),
-                g_rows[:, first : first + width],
+                planes[e][:, t, first - e * C1 : last - e * C1],
+                dc[t][:].indirect(entries(list1, first, last)),
+                g_rows[:, first:last],
                 MULT,
             )
 
-        def round_da(e):
-            da_words[e] = held.tile([P, C1, PACK], BF16, name=f"da_words{e}", align_bytes=64)
-            nc.scalar.activation(da_words[e][:], da[e][:].rearrange("p t j -> p j t"), COPY)
+        da_words, codes, code_s, results = {}, {}, {}, {}
 
-        def multiply_w1(e, tag):
-            codes = held.tile([P, C1], U32, name=f"codes{e}", align_bytes=64)
-            code_s = held.tile([P, C1], U8, name=f"code_s{e}", align_bytes=64)
+        def round_da(u, tag):
+            first, last = UNITS[u]
+            e = first // C1
+            da_words[u] = held.tile([P, last - first, PACK], BF16, name=f"da_words{u}", tag=tag, align_bytes=64)
+            src = planes[e][:, :, first - e * C1 : last - e * C1]
+            nc.scalar.activation(da_words[u][:], src.rearrange("p t j -> p j t"), COPY)
+
+        def quantise(u):
+            first, last = UNITS[u]
+            codes[u] = held.tile([P, last - first], U32, name=f"codes{u}", tag=f"codes{u}", align_bytes=64)
+            code_s[u] = held.tile([P, last - first], U8, name=f"code_s{u}", align_bytes=64)
             nc.vector.quantize_mx(
-                out=codes[:].bitcast(FP8X4), scales=code_s[:], in_=da_words[e][:].rearrange("p j t -> p (j t)")
+                out=codes[u][:].bitcast(FP8X4), scales=code_s[u][:], in_=da_words[u][:].rearrange("p j t -> p (j t)")
             )
-            acc = psum.tile([P, KP, C1], F32, name="acc1", tag=f"bank{e}")
+
+        def multiply_w1(u, h, acc):
+            e = UNITS[u][0] // C1
+            nc.tensor.matmul_mx(
+                out=acc,
+                lhsT=w1_w[:, e, 2 * P * h : 2 * P * (h + 1)].bitcast(FP4X4),
+                lhsT_scale=w1_s[:, e, h * P : (h + 1) * P],
+                rhs=codes[u][:].bitcast(FP8X4),
+                rhs_scale=code_s[u][:],
+                start=True,
+                stop=True,
+            )
+
+        def multiply_both(u, bank):
+            width = UNITS[u][1] - UNITS[u][0]
+            acc = psum.tile([P, KP, width], F32, name="acc1", tag=f"bank{bank}")
+            both = held.tile([P, KP, width], F32, name=f"results{u}")
             for h in range(KP):
-                nc.tensor.matmul_mx(
-                    out=acc[:, h, :],
-                    lhsT=w1_w[:, e, 2 * P * h : 2 * P * (h + 1)].bitcast(FP4X4),
-                    lhsT_scale=w1_s[:, e, h * P : (h + 1) * P],
-                    rhs=codes[:].bitcast(FP8X4),
-                    rhs_scale=code_s[:],
-                    start=True,
-                    stop=True,
-                )
-            results[e] = held.tile([P, KP, C1], F32, name=f"results{e}", tag=tag, align_bytes=64)
-            nc.scalar.activation(results[e][:], acc[:], COPY)
+                multiply_w1(u, h, acc[:, h, :])
+                results[u, h] = both[:, h, :]
+            nc.scalar.activation(both[:], acc[:], COPY)
+
+        def multiply_half(u, h, bank):
+            acc = psum.tile([P, C1], F32, name="acc1", tag=f"bank{bank}")
+            multiply_w1(u, h, acc[:])
+            return acc
+
+        def copy_half(u, h, acc, target):
+            results[u, h] = target
+            nc.scalar.activation(target, acc[:], COPY)
 
         dx = [held.tile([P, T], F32, name=f"dx{h}") for h in range(KP)]
 
-        def scatter_dx(e):
-            for h in range(KP):
-                nc.vector.tensor_copy(dx[h][:].indirect(entries(list1, e * C1, (e + 1) * C1)), results[e][:, h, :])
+        def scatter_dx(u, h):
+            nc.vector.tensor_copy(dx[h][:].indirect(entries(list1, *UNITS[u])), results[u, h])
 
-        for c in range(3):
-            for t in range(PACK):
-                scatter_dc(c, t)
-        da_tile(0, "da0")
-        for t in range(2):
-            scatter_dc(3, t)
-        for t in range(2):
-            for part in range(2):
-                gather_dc(0, t, part, 2)
-                scatter_dc(3, 2 + part, t, 2)
-        for t in range(2, PACK):
-            gather_dc(0, t)
-        round_da(0)
-        da_tile(1, "sums3")
-        for t in range(PACK):
-            gather_dc(1, t)
-        round_da(1)
-        multiply_w1(0, "sums3")
-        da_tile(2, "da0")
-        for t in range(PACK):
-            gather_dc(2, t)
-        round_da(2)
-        multiply_w1(1, "da0")
-        scatter_dx(0)
-        multiply_w1(2, "results2")
-        scatter_dx(1)
-        scatter_dx(2)
+        for c in range(T // PIECE):
+            for t in range(2):
+                gather_dc(t, c * PIECE, (c + 1) * PIECE)
+                scatter_dc(2 + t, late[c][:, t, :], c * PIECE, (c + 1) * PIECE)
+        gather_dc(2, 0, C1)
+        gather_dc(3, *UNITS[0])
+        round_da(0, "da_words0")
+        gather_dc(3, *UNITS[1])
+        round_da(1, "da_words1")
+        gather_dc(2, *UNITS[2])
+        gather_dc(3, *UNITS[2])
+        quantise(0)
+        multiply_both(0, 0)
+        gather_dc(2, *UNITS[3])
+        quantise(1)
+        round_da(2, "codes0")
+        multiply_both(1, 1)
+        gather_dc(3, *UNITS[3])
+        scatter_dx(0, 0)
+        scatter_dx(0, 1)
+        quantise(2)
+        halves = [multiply_half(2, h, 2 + h) for h in range(KP)]
+        wide = held.tile([P, 3, C1], F32, name="wide")
+        copy_half(2, 0, halves[0], wide[:, 0, :])
+        round_da(3, "codes2")
+        copy_half(2, 1, halves[1], da[:, :C1])
+        scatter_dx(1, 0)
+        scatter_dx(1, 1)
+        scatter_dx(2, 0)
+        quantise(3)
+        for h in range(KP):
+            copy_half(3, h, multiply_half(3, h, 4 + h), wide[:, 1 + h, :])
+        scatter_dx(2, 1)
+        scatter_dx(3, 0)
+        scatter_dx(3, 1)
 
         for h in range(KP):
             nc.sync.dma_start(out=out[h * P : (h + 1) * P, :], in_=dx[h][:])

@@ -260,10 +260,10 @@ def tile_moe_seb_none_kernel(
         def scatter_dx(u, h):
             nc.vector.tensor_copy(dx[h][:].indirect(entries(list1, *UNITS[u])), results[u, h])
 
-        for c in range(T // PIECE):
+        for first in range(0, T, C2):
             for t in range(2):
-                gather_dc(t, c * PIECE, (c + 1) * PIECE)
-                scatter_dc(2 + t, late[c][:, t, :], c * PIECE, (c + 1) * PIECE)
+                gather_dc(t, first, first + C2)
+                scatter_dc(2 + t, late[first // PIECE][:, t, first % PIECE : first % PIECE + C2], first, first + C2)
         gather_dc(2, 0, C1)
         gather_dc(3, *UNITS[0])
         round_da(0, "da_words0")

@@ -43,8 +43,8 @@ def tile_moe_seb_none_kernel(
 
         list2 = held.tile([P, T // LIST], U16, name="list2")
         list1 = held.tile([P, T // LIST], U16, name="list1")
-        dy_w = held.tile([P, WINDOW], U32, name="dy_w", tag="dy_w", align_bytes=64)
-        dy_s = held.tile([P, T], U8, name="dy_s", align_bytes=64)
+        dy_w = held.tile([P, T], U32, name="dy_w", align_bytes=64)
+        dy_s = held.tile([P, WINDOW], U8, name="dy_s", align_bytes=64)
         w2_s = [held.tile([P, H], U8, name=f"w2_s{a}", align_bytes=64) for a in range(2)]
         w1_s = held.tile([P, E1, K], U8, name="w1_s", align_bytes=64)
         w1_w = held.tile([P, E1, 2 * K], U8, name="w1_w", align_bytes=64)
@@ -79,14 +79,15 @@ def tile_moe_seb_none_kernel(
         for q in range(4):
             rows = dy_scales[0, 4 * q : 4 * q + 4, :].bitcast(I32)
             (nc.sync, nc.scalar)[q // 2].dma_start(
-                out=dy_s[32 * q : 32 * q + 32, :].bitcast(I32), in_=rows.unsqueeze(0).to_broadcast([8, 4, T // 4])
+                out=dy_s[32 * q : 32 * q + 32, :T].bitcast(I32), in_=rows.unsqueeze(0).to_broadcast([8, 4, T // 4])
             )
-        nc.sync.dma_start(out=dy_w[:, :T].bitcast(I32), in_=dy_words[0].rearrange("p t d -> p (t d)").bitcast(I32))
-        load_w2_words(0, 2)
+        nc.sync.dma_start(out=dy_w[:].bitcast(I32), in_=dy_words[0].rearrange("p t d -> p (t d)").bitcast(I32))
+        load_w2_words(0, 1)
         load_w2_scales(0, 4)
+        load_w2_words(1, 2)
         load_q_rows(0, 2)
-        load_w2_words(2, 3)
-        load_w2_words(3, E2)
+        load_w2_words(2, 4)
+        load_w2_words(4, E2)
         load_w2_scales(4, E2)
         load_q_rows(2, E2)
         nc.sync.dma_start(out=g_rows[:], in_=gate1)
@@ -98,14 +99,13 @@ def tile_moe_seb_none_kernel(
         make_identity(nc, identity[:])
 
         slot_w, slot_s = {}, {}
-        for table, dtype, by_expert, first, last, tag in (
-            (dy_s, U8, slot_s, 0, 4 * C2, "slot_s0"),
-            (dy_w, U32, slot_w, 0, C2, "slot_w0"),
-            (dy_w, U32, slot_w, C2, 2 * C2, "slot_w1"),
-            (dy_w, U32, slot_w, 2 * C2, T, "slot_w2"),
-            (dy_s, U8, slot_s, 4 * C2, T, "dy_w"),
+        for table, dtype, by_expert, first, last in (
+            (dy_s, U8, slot_s, 0, T),
+            (dy_w, U32, slot_w, 0, C2),
+            (dy_w, U32, slot_w, C2, 2 * C2),
+            (dy_w, U32, slot_w, 2 * C2, T),
         ):
-            tile = held.tile([P, last - first], dtype, name=f"slots{first}", tag=tag, align_bytes=64)
+            tile = held.tile([P, last - first], dtype, name=f"slots{first}_{last}", align_bytes=64)
             nc.vector.tensor_copy(tile[:], table[:].indirect(entries(list2, first, last)))
             for f in range(first // C2, last // C2):
                 by_expert[f] = tile[:, f * C2 - first : (f + 1) * C2 - first]
@@ -127,60 +127,67 @@ def tile_moe_seb_none_kernel(
                 start=True,
                 stop=True,
             )
-            rows[f] = held.tile([P, PACK, P], F32, name=f"rows{f}")
             products[f] = acc[:].rearrange("m (p t) -> m t p", t=PACK)
 
-        def copy_rows(f, t0, t1):
-            nc.scalar.activation(rows[f][:, t0:t1, :], products[f][:, t0:t1, :], COPY)
+        def copy_rows(f, t0):
+            rows[f] = held.tile([P, 2, P], F32, name=f"rows{f}_{t0}", tag=f"rows{f}")
+            nc.scalar.activation(rows[f][:], products[f][:, t0 : t0 + 2, :], COPY)
 
-        def turn(experts, t0, bank, target):
+        def turn(experts, bank, target):
             turned = psum.tile([P, 2, len(experts) * C2], F32, name="turned", tag=f"bank{bank}")
             for t in range(2):
                 for n, f in enumerate(experts):
-                    nc.tensor.transpose(turned[:, t, n * C2 : (n + 1) * C2], rows[f][:, t0 + t, :], identity[:])
+                    nc.tensor.transpose(turned[:, t, n * C2 : (n + 1) * C2], rows[f][:, t, :], identity[:])
             nc.scalar.activation(target, turned[:], COPY)
 
-        def first_planes(banks):
-            for t, bank in enumerate(banks):
-                words = held.tile([P, P], U32, name=f"plane_w{t}", align_bytes=64)
-                nc.gpsimd.tensor_copy(words[:], w2_w[0][:, t:H:PACK])
-                scales = held.tile([P, P], U8, name=f"plane_s{t}", align_bytes=64)
-                nc.gpsimd.tensor_copy(scales[:], w2_s[0][:, t:H:PACK])
-                acc = psum.tile([P, C2], F32, name="plane", tag=f"bank{bank}")
-                nc.tensor.matmul_mx(
-                    out=acc[:],
-                    lhsT=words[:].bitcast(FP8X4),
-                    lhsT_scale=scales[:],
-                    rhs=slot_w[0].bitcast(FP8X4),
-                    rhs_scale=slot_s[0],
-                    start=True,
-                    stop=True,
-                )
-                nc.scalar.activation(early[0][:, t, :], acc[:], COPY)
+        plane_w = [held.tile([P, 2, P], U32, name=f"plane_w{f}", align_bytes=64) for f in range(2)]
+        plane_s = [held.tile([P, P], U8, name=f"plane_s{t}", align_bytes=64) for t in range(2)]
 
-        first_planes((0, 1))
-        multiply_w2(1, 2)
-        copy_rows(1, 0, 2)
-        turn((1,), 0, 3, early[1][:])
+        def reorder_words(f):
+            nc.gpsimd.tensor_copy(plane_w[f][:], w2_w[f].rearrange("p (m t) -> p t m", t=PACK)[:, :2, :])
+
+        def short_plane(f, t, bank):
+            acc = psum.tile([P, C2], F32, name="plane", tag=f"bank{bank}")
+            nc.tensor.matmul_mx(
+                out=acc[:],
+                lhsT=plane_w[f][:, t, :].bitcast(FP8X4),
+                lhsT_scale=plane_s[t][4 * f :, :],
+                rhs=slot_w[f].bitcast(FP8X4),
+                rhs_scale=slot_s[f],
+                start=True,
+                stop=True,
+            )
+            nc.scalar.activation(early[f][:, t, :], acc[:], COPY)
+
+        reorder_words(0)
+        for t in range(2):
+            nc.gpsimd.tensor_copy(plane_s[t][:], w2_s[0][:, t:H:PACK])
+        reorder_words(1)
+        for f in range(2):
+            for t in range(2):
+                short_plane(f, t, 2 * f + t)
         multiply_w2(2, 0)
-        copy_rows(2, 0, PACK)
-        turn((2,), 0, 4, early[2][:])
+        copy_rows(2, 0)
+        turn((2,), 4, early[2][:])
         multiply_w2(3, 1)
-        copy_rows(3, 0, PACK)
-        turn((3,), 0, 3, early[3][:])
-        multiply_w2(4, 0)
-        copy_rows(4, 0, PACK)
-        turn((4,), 0, 4, early[4][:])
-        copy_rows(1, 2, PACK)
-        multiply_w2(0, 1)
-        copy_rows(0, 2, PACK)
-        multiply_w2(5, 0)
-        copy_rows(5, 0, PACK)
-        turn((0, 1), 2, 5, late[0][:])
+        copy_rows(3, 0)
+        turn((3,), 5, early[3][:])
+        multiply_w2(4, 4)
+        copy_rows(4, 0)
+        turn((4,), 6, early[4][:])
+        multiply_w2(0, 3)
+        copy_rows(0, 2)
+        multiply_w2(1, 2)
+        copy_rows(1, 2)
+        multiply_w2(5, 5)
+        copy_rows(5, 0)
+        turn((0, 1), 7, late[0][:])
         last = shared.tile([P, 2, C2], F32, name="last", offset=4 * (T - C2))
-        turn((5,), 0, 5, last[:])
-        turn((2, 3), 2, 4, late[1][:])
-        turn((4, 5), 2, 3, late[2][:])
+        turn((5,), 7, last[:])
+        for c in range(1, T // PIECE):
+            copy_rows(2 * c, 2)
+            copy_rows(2 * c + 1, 2)
+            turn((2 * c, 2 * c + 1), (6, 3)[c - 1], late[c][:])
         early.append(last)
 
         dc = [held.tile([P, T], F32, name=f"dc{t}") for t in range(2)]
@@ -247,7 +254,7 @@ def tile_moe_seb_none_kernel(
             nc.scalar.activation(both[:], acc[:], COPY)
 
         def multiply_half(u, h, bank):
-            acc = psum.tile([P, C1], F32, name="acc1", tag=f"bank{bank}")
+            acc = psum.tile([P, UNITS[u][1] - UNITS[u][0]], F32, name="acc1", tag=f"bank{bank}")
             multiply_w1(u, h, acc[:])
             return acc
 
@@ -255,6 +262,7 @@ def tile_moe_seb_none_kernel(
             results[u, h] = target
             nc.scalar.activation(target, acc[:], COPY)
 
+        first_results = held.tile([P, KP, C2], F32, name="first_results")
         dx = [held.tile([P, T], F32, name=f"dx{h}") for h in range(KP)]
 
         def scatter_dx(u, h):
@@ -272,7 +280,8 @@ def tile_moe_seb_none_kernel(
         gather_dc(2, *UNITS[2])
         gather_dc(3, *UNITS[2])
         quantise(0)
-        multiply_both(0, 0)
+        for h in range(KP):
+            copy_half(0, h, multiply_half(0, h, 6 + h), first_results[:, h, :])
         gather_dc(2, *UNITS[3])
         quantise(1)
         round_da(2, "codes0")

@@ -22,9 +22,7 @@ P = 128
 LIST = 16
 PACK = 4
 KP = K // P
-GROUPS = ((0, 1), (1, 2), (2, 3), (3, 4), (4, 5), (5, 6))
 UNITS = ((0, 128), (128, 256), (256, 512), (512, 768))
-WINDOW = 1024
 PIECE = 256
 
 
@@ -44,7 +42,7 @@ def tile_moe_seb_none_kernel(
         list2 = held.tile([P, T // LIST], U16, name="list2")
         list1 = held.tile([P, T // LIST], U16, name="list1")
         dy_w = held.tile([P, T], U32, name="dy_w", align_bytes=64)
-        dy_s = held.tile([P, WINDOW], U8, name="dy_s", align_bytes=64)
+        dy_s = held.tile([P, T], U8, name="dy_s", align_bytes=64)
         w2_s = [held.tile([P, H], U8, name=f"w2_s{a}", align_bytes=64) for a in range(2)]
         w1_s = held.tile([P, E1, K], U8, name="w1_s", align_bytes=64)
         w1_w = held.tile([P, E1, 2 * K], U8, name="w1_w", align_bytes=64)
@@ -79,7 +77,7 @@ def tile_moe_seb_none_kernel(
         for q in range(4):
             rows = dy_scales[0, 4 * q : 4 * q + 4, :].bitcast(I32)
             (nc.sync, nc.scalar)[q // 2].dma_start(
-                out=dy_s[32 * q : 32 * q + 32, :T].bitcast(I32), in_=rows.unsqueeze(0).to_broadcast([8, 4, T // 4])
+                out=dy_s[32 * q : 32 * q + 32, :].bitcast(I32), in_=rows.unsqueeze(0).to_broadcast([8, 4, T // 4])
             )
         nc.sync.dma_start(out=dy_w[:].bitcast(I32), in_=dy_words[0].rearrange("p t d -> p (t d)").bitcast(I32))
         load_w2_words(0, 1)
@@ -99,20 +97,23 @@ def tile_moe_seb_none_kernel(
         make_identity(nc, identity[:])
 
         slot_w, slot_s = {}, {}
-        for table, dtype, by_expert, first, last in (
-            (dy_s, U8, slot_s, 0, T),
-            (dy_w, U32, slot_w, 0, C2),
-            (dy_w, U32, slot_w, C2, 2 * C2),
-            (dy_w, U32, slot_w, 2 * C2, T),
-        ):
-            tile = held.tile([P, last - first], dtype, name=f"slots{first}_{last}", align_bytes=64)
-            nc.vector.tensor_copy(tile[:], table[:].indirect(entries(list2, first, last)))
-            for f in range(first // C2, last // C2):
-                by_expert[f] = tile[:, f * C2 - first : (f + 1) * C2 - first]
 
-        early = [
-            held.tile([P, 2, (f1 - f0) * C2], F32, name=f"early{f0}") for f0, f1 in GROUPS[:-1]
-        ]
+        def gather_slots(table, dtype, by_expert, f0, f1, tag):
+            tile = held.tile([P, (f1 - f0) * C2], dtype, name=tag, tag=tag, align_bytes=64)
+            nc.vector.tensor_copy(tile[:], table[:].indirect(entries(list2, f0 * C2, f1 * C2)))
+            for f in range(f0, f1):
+                by_expert[f] = tile[:, (f - f0) * C2 : (f - f0 + 1) * C2]
+
+        gather_slots(dy_s, U8, slot_s, 0, 4, "slot_s0")
+        gather_slots(dy_w, U32, slot_w, 0, 1, "slot_w0")
+        gather_slots(dy_w, U32, slot_w, 1, 2, "slot_w1")
+        gather_slots(dy_w, U32, slot_w, 2, E2, "slot_w2")
+
+        early = {
+            (f, t): held.tile([P, C2], F32, name=f"early{f}_{t}", tag=f"early{f}_{t}", align_bytes=64)[:]
+            for f in range(2)
+            for t in range(2)
+        }
         late = [held.tile([P, 2, PIECE], F32, name=f"late{c}") for c in range(T // PIECE)]
         rows, products = {}, {}
 
@@ -157,38 +158,7 @@ def tile_moe_seb_none_kernel(
                 start=True,
                 stop=True,
             )
-            nc.scalar.activation(early[f][:, t, :], acc[:], COPY)
-
-        reorder_words(0)
-        for t in range(2):
-            nc.gpsimd.tensor_copy(plane_s[t][:], w2_s[0][:, t:H:PACK])
-        reorder_words(1)
-        for f in range(2):
-            for t in range(2):
-                short_plane(f, t, 2 * f + t)
-        multiply_w2(2, 0)
-        copy_rows(2, 0)
-        turn((2,), 4, early[2][:])
-        multiply_w2(3, 1)
-        copy_rows(3, 0)
-        turn((3,), 5, early[3][:])
-        multiply_w2(4, 4)
-        copy_rows(4, 0)
-        turn((4,), 6, early[4][:])
-        multiply_w2(0, 3)
-        copy_rows(0, 2)
-        multiply_w2(1, 2)
-        copy_rows(1, 2)
-        multiply_w2(5, 5)
-        copy_rows(5, 0)
-        turn((0, 1), 7, late[0][:])
-        last = shared.tile([P, 2, C2], F32, name="last", offset=4 * (T - C2))
-        turn((5,), 7, last[:])
-        for c in range(1, T // PIECE):
-            copy_rows(2 * c, 2)
-            copy_rows(2 * c + 1, 2)
-            turn((2 * c, 2 * c + 1), (6, 3)[c - 1], late[c][:])
-        early.append(last)
+            nc.scalar.activation(early[f, t], acc[:], COPY)
 
         dc = [held.tile([P, T], F32, name=f"dc{t}") for t in range(2)]
 
@@ -197,9 +167,46 @@ def tile_moe_seb_none_kernel(
                 dc[t][:].indirect(entries(list2, first, last)), sums, q_rows[:, first:last], MULT
             )
 
-        for c, (f0, f1) in enumerate(GROUPS):
+        reorder_words(0)
+        for t in range(2):
+            nc.gpsimd.tensor_copy(plane_s[t][:], w2_s[0][:, t:H:PACK])
+        reorder_words(1)
+        for f in range(2):
             for t in range(2):
-                scatter_dc(t, early[c][:, t, :], f0 * C2, f1 * C2)
+                short_plane(f, t, 2 * f + t)
+        for t in range(2):
+            scatter_dc(t, early[0, t], 0, C2)
+        for t in range(2):
+            scatter_dc(t, early[1, t], C2, 2 * C2)
+            gather_slots(dy_s, U8, slot_s, 4 + t, 5 + t, ("early0_1", "early1_0")[t])
+
+        def turn_early(f, bank, tile):
+            turn((f,), bank, tile[:])
+            for t in range(2):
+                scatter_dc(t, tile[:, t, :], f * C2, (f + 1) * C2)
+
+        multiply_w2(2, 0)
+        copy_rows(2, 0)
+        turn_early(2, 4, held.tile([P, 2, C2], F32, name="early2"))
+        multiply_w2(3, 1)
+        copy_rows(3, 0)
+        turn_early(3, 5, held.tile([P, 2, C2], F32, name="early3"))
+        multiply_w2(4, 4)
+        copy_rows(4, 0)
+        turn_early(4, 6, held.tile([P, 2, C2], F32, name="early4"))
+        multiply_w2(0, 3)
+        copy_rows(0, 2)
+        multiply_w2(1, 2)
+        copy_rows(1, 2)
+        multiply_w2(5, 5)
+        copy_rows(5, 0)
+        turn((0, 1), 7, late[0][:])
+        last = shared.tile([P, 2, C2], F32, name="last", offset=4 * (T - C2))
+        turn_early(5, 7, last)
+        for c in range(1, T // PIECE):
+            copy_rows(2 * c, 2)
+            copy_rows(2 * c + 1, 2)
+            turn((2 * c, 2 * c + 1), (6, 3)[c - 1], late[c][:])
         dc.extend(shared.tile([P, T], F32, name=f"dc{2 + t}", offset=4 * T * t) for t in range(2))
 
         starts = (2 * C1 + C1 // 2, 6 * C1 + C1 // 2, 0)

@@ -1,7 +1,6 @@
 from contextlib import ExitStack
 
 import concourse.mybir as mybir
-from concourse.masks import make_identity
 
 K, T, H, N = 256, 768, 512, 512
 E1, C1, E2, C2 = 3, 256, 6, 128
@@ -23,7 +22,6 @@ LIST = 16
 PACK = 4
 KP = K // P
 UNITS = ((0, 128), (128, 256), (256, 512), (512, 768))
-PIECE = 256
 
 
 def entries(offsets, first, last):
@@ -36,7 +34,6 @@ def tile_moe_seb_none_kernel(
     nc = tc.nc
     with ExitStack() as ctx:
         held = ctx.enter_context(tc.tile_pool(name="held", bufs=1))
-        shared = ctx.enter_context(tc.tile_pool(name="shared", bufs=1))
         psum = ctx.enter_context(tc.psum_pool(name="psum", bufs=1))
 
         list2 = held.tile([P, T // LIST], U16, name="list2")
@@ -48,7 +45,6 @@ def tile_moe_seb_none_kernel(
         w1_w = held.tile([P, E1, 2 * K], U8, name="w1_w", align_bytes=64)
         q_rows = held.tile([P, T], F32, name="q_rows")
         g_rows = held.tile([P, T], F32, name="g_rows")
-        identity = held.tile([P, P], F32, name="identity")
 
         nc.vector.memset(w2_s[0][:].bitcast(I32), 0)
         nc.vector.memset(w2_s[1][:].bitcast(I32), 0)
@@ -94,7 +90,6 @@ def tile_moe_seb_none_kernel(
         for r in range(4):
             nc.sync.dma_start(out=w1_s[r:P:32].bitcast(I32), in_=w1_rows[r].bitcast(I32))
         nc.sync.dma_start(out=w1_w[:].bitcast(I32), in_=w1t_words[:, 0].rearrange("e p c -> p e c").bitcast(I32))
-        make_identity(nc, identity[:])
 
         slot_w, slot_s = {}, {}
 
@@ -104,213 +99,156 @@ def tile_moe_seb_none_kernel(
             for f in range(f0, f1):
                 by_expert[f] = tile[:, (f - f0) * C2 : (f - f0 + 1) * C2]
 
-        gather_slots(dy_s, U8, slot_s, 0, 4, "slot_s0")
+        plane_w = [held.tile([P, PACK, P], U32, name=f"plane_w{f}", align_bytes=64) for f in range(E2)]
+        plane_s = [held.tile([P, PACK, P], U8, name=f"plane_s{a}", align_bytes=64) for a in range(2)]
+
+        def reorder_words(f, copy):
+            copy(plane_w[f][:], w2_w[f].rearrange("p (m t) -> p t m", t=PACK))
+
+        def reorder_scales(a):
+            nc.gpsimd.tensor_copy(plane_s[a][:], w2_s[a][:].rearrange("p (m t) -> p t m", t=PACK))
+
+        sums = [held.tile([P, PACK, 2 * C2], F32, name=f"sums{c}") for c in range(E2 // 2)]
+
+        def multiply_w2(f, t0, t1, bank):
+            acc = psum.tile([P, t1 - t0, C2], F32, name="acc2", tag=f"bank{bank}")
+            for t in range(t0, t1):
+                nc.tensor.matmul_mx(
+                    out=acc[:, t - t0, :],
+                    lhsT=plane_w[f][:, t, :].bitcast(FP8X4),
+                    lhsT_scale=plane_s[f // 4][4 * (f % 4) :, t, :],
+                    rhs=slot_w[f].bitcast(FP8X4),
+                    rhs_scale=slot_s[f],
+                    start=True,
+                    stop=True,
+                )
+            gate = q_rows[:, f * C2 : (f + 1) * C2].unsqueeze(1).to_broadcast([P, t1 - t0, C2])
+            nc.vector.tensor_tensor(sums[f // 2][:, t0:t1, (f % 2) * C2 : (f % 2 + 1) * C2], acc[:], gate, MULT)
+
+        dc = [held.tile([P, T], F32, name=f"dc{t}") for t in range(PACK)]
+
+        def on_scalar(dst, src):
+            nc.scalar.activation(dst, src, COPY)
+
+        on_vector = nc.vector.tensor_copy
+
+        def scatter_dc(copy, t, f0, f1):
+            src = sums[f0 // 2][:, t, (f0 % 2) * C2 : (f0 % 2 + f1 - f0) * C2]
+            copy(dc[t][:].indirect(entries(list2, f0 * C2, f1 * C2)), src)
+
+        gather_slots(dy_s, U8, slot_s, 0, 2, "slot_s0")
         gather_slots(dy_w, U32, slot_w, 0, 1, "slot_w0")
         gather_slots(dy_w, U32, slot_w, 1, 2, "slot_w1")
-        gather_slots(dy_w, U32, slot_w, 2, E2, "slot_w2")
+        reorder_words(0, nc.scalar.copy)
+        reorder_scales(0)
+        reorder_words(1, nc.scalar.copy)
+        multiply_w2(0, 0, 2, 0)
+        gather_slots(dy_s, U8, slot_s, 2, 4, "slot_s2")
+        multiply_w2(0, 2, 4, 1)
+        gather_slots(dy_w, U32, slot_w, 2, 4, "slot_w2")
+        scatter_dc(on_scalar, 0, 0, 1)
+        scatter_dc(on_scalar, 1, 0, 1)
+        multiply_w2(1, 0, 4, 2)
+        scatter_dc(on_scalar, 0, 1, 2)
+        scatter_dc(on_scalar, 1, 1, 2)
+        reorder_words(2, nc.gpsimd.tensor_copy)
+        reorder_words(3, nc.gpsimd.tensor_copy)
+        reorder_words(4, nc.gpsimd.tensor_copy)
+        reorder_scales(1)
+        reorder_words(5, nc.gpsimd.tensor_copy)
+        gather_slots(dy_s, U8, slot_s, 4, 6, "slot_s4")
+        multiply_w2(2, 0, 4, 3)
+        gather_slots(dy_w, U32, slot_w, 4, 6, "slot_w4")
+        multiply_w2(3, 0, 4, 4)
+        scatter_dc(on_scalar, 0, 2, 4)
+        scatter_dc(on_scalar, 1, 2, 4)
+        scatter_dc(on_vector, 2, 0, 2)
+        multiply_w2(4, 0, 4, 5)
+        scatter_dc(on_vector, 3, 0, 1)
+        multiply_w2(5, 0, 4, 6)
+        scatter_dc(on_vector, 2, 2, 4)
+        scatter_dc(on_scalar, 0, 4, 6)
+        scatter_dc(on_scalar, 1, 4, 6)
+        scatter_dc(on_scalar, 3, 1, 2)
+        scatter_dc(on_scalar, 3, 2, 4)
+        scatter_dc(on_scalar, 3, 4, 6)
 
-        early = {
-            (f, t): held.tile([P, C2], F32, name=f"early{f}_{t}", tag=f"early{f}_{t}", align_bytes=64)[:]
-            for f in range(2)
-            for t in range(2)
-        }
-        late = [held.tile([P, 2, PIECE], F32, name=f"late{c}") for c in range(T // PIECE)]
-        rows, products = {}, {}
+        da = [held.tile([P, PACK, last - first], F32, name=f"da{u}") for u, (first, last) in enumerate(UNITS)]
 
-        def multiply_w2(f, bank):
-            acc = psum.tile([P, H], F32, name="acc2", tag=f"bank{bank}")
-            nc.tensor.matmul_mx(
-                out=acc[:],
-                lhsT=slot_w[f].bitcast(FP8X4),
-                lhsT_scale=slot_s[f],
-                rhs=w2_w[f].bitcast(FP8X4),
-                rhs_scale=w2_s[f // 4][4 * (f % 4) :, :],
-                start=True,
-                stop=True,
-            )
-            products[f] = acc[:].rearrange("m (p t) -> m t p", t=PACK)
-
-        def copy_rows(f, t0):
-            rows[f] = held.tile([P, 2, P], F32, name=f"rows{f}_{t0}", tag=f"rows{f}")
-            nc.scalar.activation(rows[f][:], products[f][:, t0 : t0 + 2, :], COPY)
-
-        def turn(experts, bank, target):
-            turned = psum.tile([P, 2, len(experts) * C2], F32, name="turned", tag=f"bank{bank}")
-            for t in range(2):
-                for n, f in enumerate(experts):
-                    nc.tensor.transpose(turned[:, t, n * C2 : (n + 1) * C2], rows[f][:, t, :], identity[:])
-            nc.scalar.activation(target, turned[:], COPY)
-
-        plane_w = [held.tile([P, 2, P], U32, name=f"plane_w{f}", align_bytes=64) for f in range(2)]
-        plane_s = [held.tile([P, P], U8, name=f"plane_s{t}", align_bytes=64) for t in range(2)]
-
-        def reorder_words(f):
-            nc.gpsimd.tensor_copy(plane_w[f][:], w2_w[f].rearrange("p (m t) -> p t m", t=PACK)[:, :2, :])
-
-        def short_plane(f, t, bank):
-            acc = psum.tile([P, C2], F32, name="plane", tag=f"bank{bank}")
-            nc.tensor.matmul_mx(
-                out=acc[:],
-                lhsT=plane_w[f][:, t, :].bitcast(FP8X4),
-                lhsT_scale=plane_s[t][4 * f :, :],
-                rhs=slot_w[f].bitcast(FP8X4),
-                rhs_scale=slot_s[f],
-                start=True,
-                stop=True,
-            )
-            nc.scalar.activation(early[f, t], acc[:], COPY)
-
-        dc = [held.tile([P, T], F32, name=f"dc{t}") for t in range(2)]
-
-        def scatter_dc(t, sums, first, last):
+        def gather_dc(t, u):
+            first, last = UNITS[u]
             nc.vector.tensor_tensor(
-                dc[t][:].indirect(entries(list2, first, last)), sums, q_rows[:, first:last], MULT
-            )
-
-        reorder_words(0)
-        for t in range(2):
-            nc.gpsimd.tensor_copy(plane_s[t][:], w2_s[0][:, t:H:PACK])
-        reorder_words(1)
-        for f in range(2):
-            for t in range(2):
-                short_plane(f, t, 2 * f + t)
-        for t in range(2):
-            scatter_dc(t, early[0, t], 0, C2)
-        for t in range(2):
-            scatter_dc(t, early[1, t], C2, 2 * C2)
-            gather_slots(dy_s, U8, slot_s, 4 + t, 5 + t, ("early0_1", "early1_0")[t])
-
-        def turn_early(f, bank, tile):
-            turn((f,), bank, tile[:])
-            for t in range(2):
-                scatter_dc(t, tile[:, t, :], f * C2, (f + 1) * C2)
-
-        multiply_w2(2, 0)
-        copy_rows(2, 0)
-        turn_early(2, 4, held.tile([P, 2, C2], F32, name="early2"))
-        multiply_w2(3, 1)
-        copy_rows(3, 0)
-        turn_early(3, 5, held.tile([P, 2, C2], F32, name="early3"))
-        multiply_w2(4, 4)
-        copy_rows(4, 0)
-        turn_early(4, 6, held.tile([P, 2, C2], F32, name="early4"))
-        multiply_w2(0, 3)
-        copy_rows(0, 2)
-        multiply_w2(1, 2)
-        copy_rows(1, 2)
-        multiply_w2(5, 5)
-        copy_rows(5, 0)
-        turn((0, 1), 7, late[0][:])
-        last = shared.tile([P, 2, C2], F32, name="last", offset=4 * (T - C2))
-        turn_early(5, 7, last)
-        for c in range(1, T // PIECE):
-            copy_rows(2 * c, 2)
-            copy_rows(2 * c + 1, 2)
-            turn((2 * c, 2 * c + 1), (6, 3)[c - 1], late[c][:])
-        dc.extend(shared.tile([P, T], F32, name=f"dc{2 + t}", offset=4 * T * t) for t in range(2))
-
-        starts = (2 * C1 + C1 // 2, 6 * C1 + C1 // 2, 0)
-        da = held.tile([P, starts[1] + PACK * C1], F32, name="da", align_bytes=64)
-        planes = [da[:, s : s + PACK * C1].rearrange("p (t j) -> p t j", t=PACK) for s in starts]
-
-        def gather_dc(t, first, last):
-            e = first // C1
-            nc.vector.tensor_tensor(
-                planes[e][:, t, first - e * C1 : last - e * C1],
-                dc[t][:].indirect(entries(list1, first, last)),
-                g_rows[:, first:last],
-                MULT,
+                da[u][:, t, :], dc[t][:].indirect(entries(list1, first, last)), g_rows[:, first:last], MULT
             )
 
         da_words, codes, code_s, results = {}, {}, {}, {}
 
-        def round_da(u, tag):
+        def round_da(copy, u):
             first, last = UNITS[u]
-            e = first // C1
-            da_words[u] = held.tile([P, last - first, PACK], BF16, name=f"da_words{u}", tag=tag, align_bytes=64)
-            src = planes[e][:, :, first - e * C1 : last - e * C1]
-            nc.scalar.activation(da_words[u][:], src.rearrange("p t j -> p j t"), COPY)
+            da_words[u] = held.tile([P, last - first, PACK], BF16, name=f"da_words{u}", align_bytes=64)
+            copy(da_words[u][:], da[u][:].rearrange("p t j -> p j t"))
 
         def quantise(u):
             first, last = UNITS[u]
-            codes[u] = held.tile([P, last - first], U32, name=f"codes{u}", tag=f"codes{u}", align_bytes=64)
+            codes[u] = held.tile([P, last - first], U32, name=f"codes{u}", align_bytes=64)
             code_s[u] = held.tile([P, last - first], U8, name=f"code_s{u}", align_bytes=64)
             nc.vector.quantize_mx(
                 out=codes[u][:].bitcast(FP8X4), scales=code_s[u][:], in_=da_words[u][:].rearrange("p j t -> p (j t)")
             )
 
-        def multiply_w1(u, h, acc):
-            e = UNITS[u][0] // C1
-            nc.tensor.matmul_mx(
-                out=acc,
-                lhsT=w1_w[:, e, 2 * P * h : 2 * P * (h + 1)].bitcast(FP4X4),
-                lhsT_scale=w1_s[:, e, h * P : (h + 1) * P],
-                rhs=codes[u][:].bitcast(FP8X4),
-                rhs_scale=code_s[u][:],
-                start=True,
-                stop=True,
-            )
-
-        def multiply_both(u, bank):
-            width = UNITS[u][1] - UNITS[u][0]
-            acc = psum.tile([P, KP, width], F32, name="acc1", tag=f"bank{bank}")
-            both = held.tile([P, KP, width], F32, name=f"results{u}")
+        def multiply_w1(u, bank):
+            first, last = UNITS[u]
+            e = first // C1
+            acc = psum.tile([P, KP, last - first], F32, name="acc1", tag=f"bank{bank}")
             for h in range(KP):
-                multiply_w1(u, h, acc[:, h, :])
-                results[u, h] = both[:, h, :]
-            nc.scalar.activation(both[:], acc[:], COPY)
+                nc.tensor.matmul_mx(
+                    out=acc[:, h, :],
+                    lhsT=w1_w[:, e, 2 * P * h : 2 * P * (h + 1)].bitcast(FP4X4),
+                    lhsT_scale=w1_s[:, e, h * P : (h + 1) * P],
+                    rhs=codes[u][:].bitcast(FP8X4),
+                    rhs_scale=code_s[u][:],
+                    start=True,
+                    stop=True,
+                )
+            results[u] = held.tile([P, KP, last - first], F32, name=f"results{u}")
+            on_scalar(results[u][:], acc[:])
 
-        def multiply_half(u, h, bank):
-            acc = psum.tile([P, UNITS[u][1] - UNITS[u][0]], F32, name="acc1", tag=f"bank{bank}")
-            multiply_w1(u, h, acc[:])
-            return acc
-
-        def copy_half(u, h, acc, target):
-            results[u, h] = target
-            nc.scalar.activation(target, acc[:], COPY)
-
-        first_results = held.tile([P, KP, C2], F32, name="first_results")
         dx = [held.tile([P, T], F32, name=f"dx{h}") for h in range(KP)]
 
-        def scatter_dx(u, h):
-            nc.vector.tensor_copy(dx[h][:].indirect(entries(list1, *UNITS[u])), results[u, h])
+        def scatter_dx(copy, u, h):
+            copy(dx[h][:].indirect(entries(list1, *UNITS[u])), results[u][:, h, :])
 
-        for first in range(0, T, C2):
-            for t in range(2):
-                gather_dc(t, first, first + C2)
-                scatter_dc(2 + t, late[first // PIECE][:, t, first % PIECE : first % PIECE + C2], first, first + C2)
-        gather_dc(2, 0, C1)
-        gather_dc(3, *UNITS[0])
-        round_da(0, "da_words0")
-        gather_dc(3, *UNITS[1])
-        round_da(1, "da_words1")
-        gather_dc(2, *UNITS[2])
-        gather_dc(3, *UNITS[2])
+        gather_dc(0, 0)
+        scatter_dc(on_vector, 2, 4, 6)
+        for u in range(1, 4):
+            gather_dc(0, u)
+        for t in (1, 2):
+            for u in range(4):
+                gather_dc(t, u)
+        gather_dc(3, 0)
+        gather_dc(3, 1)
+        round_da(on_vector, 0)
+        gather_dc(3, 2)
+        round_da(on_scalar, 1)
         quantise(0)
-        for h in range(KP):
-            copy_half(0, h, multiply_half(0, h, 6 + h), first_results[:, h, :])
-        gather_dc(2, *UNITS[3])
+        round_da(on_scalar, 2)
+        gather_dc(3, 3)
+        multiply_w1(0, 7)
         quantise(1)
-        round_da(2, "codes0")
-        multiply_both(1, 1)
-        gather_dc(3, *UNITS[3])
-        scatter_dx(0, 0)
-        scatter_dx(0, 1)
+        scatter_dx(on_scalar, 0, 1)
+        round_da(on_vector, 3)
+        multiply_w1(1, 0)
         quantise(2)
-        halves = [multiply_half(2, h, 2 + h) for h in range(KP)]
-        wide = held.tile([P, 3, C1], F32, name="wide")
-        copy_half(2, 0, halves[0], wide[:, 0, :])
-        round_da(3, "codes2")
-        copy_half(2, 1, halves[1], da[:, :C1])
-        scatter_dx(1, 0)
-        scatter_dx(1, 1)
-        scatter_dx(2, 0)
+        scatter_dx(on_vector, 0, 0)
+        scatter_dx(on_scalar, 1, 1)
+        multiply_w1(2, 1)
         quantise(3)
-        for h in range(KP):
-            copy_half(3, h, multiply_half(3, h, 4 + h), wide[:, 1 + h, :])
-        scatter_dx(2, 1)
-        scatter_dx(3, 0)
-        scatter_dx(3, 1)
+        scatter_dx(on_vector, 1, 0)
+        scatter_dx(on_scalar, 2, 1)
+        multiply_w1(3, 2)
+        scatter_dx(on_vector, 2, 0)
+        scatter_dx(on_scalar, 3, 1)
+        scatter_dx(on_vector, 3, 0)
 
         for h in range(KP):
             nc.sync.dma_start(out=out[h * P : (h + 1) * P, :], in_=dx[h][:])

@@ -20,6 +20,7 @@ MULT = mybir.AluOpType.mult
 P = 128
 LIST = 16
 PACK = 4
+LINE = 4
 KP = K // P
 UNITS = ((0, 128), (128, 256), (256, 512), (512, 768))
 
@@ -99,31 +100,38 @@ def tile_moe_seb_none_kernel(
             for f in range(f0, f1):
                 by_expert[f] = tile[:, (f - f0) * C2 : (f - f0 + 1) * C2]
 
-        plane_w = [held.tile([P, PACK, P], U32, name=f"plane_w{f}", align_bytes=64) for f in range(E2)]
-        plane_s = [held.tile([P, PACK, P], U8, name=f"plane_s{a}", align_bytes=64) for a in range(2)]
+        plane_w, plane_s = {}, {}
 
-        def reorder_words(f, copy):
-            copy(plane_w[f][:], w2_w[f].rearrange("p (m t) -> p t m", t=PACK))
+        def reorder_words(copy, f, t0, t1):
+            tile = held.tile([P, t1 - t0, P], U32, name=f"plane_w{f}_{t0}", tag=f"plane_w{f}_{t0}", align_bytes=64)
+            src = w2_w[f].rearrange("p (c i t) -> p c t i", i=LINE, t=PACK)[:, :, t0:t1, :]
+            copy(tile[:].rearrange("p t (c i) -> p c t i", i=LINE), src)
+            for t in range(t0, t1):
+                plane_w[f, t] = tile[:, t - t0, :]
 
-        def reorder_scales(a):
-            nc.gpsimd.tensor_copy(plane_s[a][:], w2_s[a][:].rearrange("p (m t) -> p t m", t=PACK))
+        def reorder_scales(a, t0, t1):
+            tile = held.tile([P, t1 - t0, P], U8, name=f"plane_s{a}_{t0}", align_bytes=64)
+            nc.gpsimd.tensor_copy(tile[:], w2_s[a][:].rearrange("p (m t) -> p t m", t=PACK)[:, t0:t1, :])
+            for t in range(t0, t1):
+                plane_s[a, t] = tile
+                plane_s[a, t, "at"] = t - t0
 
-        sums = [held.tile([P, PACK, 2 * C2], F32, name=f"sums{c}") for c in range(E2 // 2)]
+        sums = held.tile([P, PACK, T], F32, name="sums")
 
         def multiply_w2(f, t0, t1, bank):
             acc = psum.tile([P, t1 - t0, C2], F32, name="acc2", tag=f"bank{bank}")
             for t in range(t0, t1):
                 nc.tensor.matmul_mx(
                     out=acc[:, t - t0, :],
-                    lhsT=plane_w[f][:, t, :].bitcast(FP8X4),
-                    lhsT_scale=plane_s[f // 4][4 * (f % 4) :, t, :],
+                    lhsT=plane_w[f, t].bitcast(FP8X4),
+                    lhsT_scale=plane_s[f // 4, t][4 * (f % 4) :, plane_s[f // 4, t, "at"], :],
                     rhs=slot_w[f].bitcast(FP8X4),
                     rhs_scale=slot_s[f],
                     start=True,
                     stop=True,
                 )
             gate = q_rows[:, f * C2 : (f + 1) * C2].unsqueeze(1).to_broadcast([P, t1 - t0, C2])
-            nc.vector.tensor_tensor(sums[f // 2][:, t0:t1, (f % 2) * C2 : (f % 2 + 1) * C2], acc[:], gate, MULT)
+            nc.vector.tensor_tensor(sums[:, t0:t1, f * C2 : (f + 1) * C2], acc[:], gate, MULT)
 
         dc = [held.tile([P, T], F32, name=f"dc{t}") for t in range(PACK)]
 
@@ -133,60 +141,59 @@ def tile_moe_seb_none_kernel(
         on_vector = nc.vector.tensor_copy
 
         def scatter_dc(copy, t, f0, f1):
-            src = sums[f0 // 2][:, t, (f0 % 2) * C2 : (f0 % 2 + f1 - f0) * C2]
-            copy(dc[t][:].indirect(entries(list2, f0 * C2, f1 * C2)), src)
+            copy(dc[t][:].indirect(entries(list2, f0 * C2, f1 * C2)), sums[:, t, f0 * C2 : f1 * C2])
 
-        gather_slots(dy_s, U8, slot_s, 0, 2, "slot_s0")
+        gather_slots(dy_s, U8, slot_s, 0, 4, "slot_s0")
         gather_slots(dy_w, U32, slot_w, 0, 1, "slot_w0")
         gather_slots(dy_w, U32, slot_w, 1, 2, "slot_w1")
-        reorder_words(0, nc.scalar.copy)
-        reorder_scales(0)
-        reorder_words(1, nc.scalar.copy)
-        multiply_w2(0, 0, 2, 0)
-        gather_slots(dy_s, U8, slot_s, 2, 4, "slot_s2")
-        multiply_w2(0, 2, 4, 1)
         gather_slots(dy_w, U32, slot_w, 2, 4, "slot_w2")
-        scatter_dc(on_scalar, 0, 0, 1)
-        scatter_dc(on_scalar, 1, 0, 1)
+        for t0 in (0, 2):
+            reorder_words(nc.scalar.copy, 0, t0, t0 + 2)
+            reorder_scales(0, t0, t0 + 2)
+        reorder_words(nc.scalar.copy, 1, 0, PACK)
+        multiply_w2(0, 0, 2, 0)
+        multiply_w2(0, 2, 4, 1)
         multiply_w2(1, 0, 4, 2)
-        scatter_dc(on_scalar, 0, 1, 2)
-        scatter_dc(on_scalar, 1, 1, 2)
-        reorder_words(2, nc.gpsimd.tensor_copy)
-        reorder_words(3, nc.gpsimd.tensor_copy)
-        reorder_words(4, nc.gpsimd.tensor_copy)
-        reorder_scales(1)
-        reorder_words(5, nc.gpsimd.tensor_copy)
-        gather_slots(dy_s, U8, slot_s, 4, 6, "slot_s4")
+        for f in range(2, 5):
+            reorder_words(nc.gpsimd.tensor_copy, f, 0, PACK)
+        reorder_scales(1, 0, PACK)
+        reorder_words(nc.gpsimd.tensor_copy, 5, 0, PACK)
+        scatter_dc(on_vector, 0, 0, 1)
+        gather_slots(dy_s, U8, slot_s, 4, 6, "slot_w1")
+        gather_slots(dy_w, U32, slot_w, 4, 6, "plane_w1_0")
         multiply_w2(2, 0, 4, 3)
-        gather_slots(dy_w, U32, slot_w, 4, 6, "slot_w4")
         multiply_w2(3, 0, 4, 4)
-        scatter_dc(on_scalar, 0, 2, 4)
-        scatter_dc(on_scalar, 1, 2, 4)
-        scatter_dc(on_vector, 2, 0, 2)
+        scatter_dc(on_vector, 0, 1, 3)
         multiply_w2(4, 0, 4, 5)
-        scatter_dc(on_vector, 3, 0, 1)
         multiply_w2(5, 0, 4, 6)
-        scatter_dc(on_vector, 2, 2, 4)
-        scatter_dc(on_scalar, 0, 4, 6)
-        scatter_dc(on_scalar, 1, 4, 6)
-        scatter_dc(on_scalar, 3, 1, 2)
-        scatter_dc(on_scalar, 3, 2, 4)
-        scatter_dc(on_scalar, 3, 4, 6)
+        scatter_dc(on_vector, 0, 3, 6)
+        for t, f0, f1 in ((1, 0, 1), (2, 0, 1), (3, 0, 1), (1, 1, 2), (2, 1, 2), (3, 1, 3)):
+            scatter_dc(on_scalar, t, f0, f1)
+        for f in (2, 4):
+            for t in (1, 2):
+                scatter_dc(on_scalar, t, f, f + 2)
+        scatter_dc(on_scalar, 3, 3, 6)
 
-        da = [held.tile([P, PACK, last - first], F32, name=f"da{u}") for u, (first, last) in enumerate(UNITS)]
+        da_first = held.tile([P, PACK, C1], F32, name="da_first", tag="da_first", align_bytes=64)
+        da_rest = held.tile([P, PACK, T - C1], F32, name="da_rest")
 
-        def gather_dc(t, u):
-            first, last = UNITS[u]
+        def da(first, last):
+            return da_first[:, :, first:last] if first < C1 else da_rest[:, :, first - C1 : last - C1]
+
+        def gather_dc(t, first, last):
             nc.vector.tensor_tensor(
-                da[u][:, t, :], dc[t][:].indirect(entries(list1, first, last)), g_rows[:, first:last], MULT
+                da(first, last)[:, t, :], dc[t][:].indirect(entries(list1, first, last)), g_rows[:, first:last], MULT
             )
 
-        da_words, codes, code_s, results = {}, {}, {}, {}
+        da_words, codes, code_s = {}, {}, {}
 
-        def round_da(copy, u):
+        def round_da(copy, u, tag):
             first, last = UNITS[u]
-            da_words[u] = held.tile([P, last - first, PACK], BF16, name=f"da_words{u}", align_bytes=64)
-            copy(da_words[u][:], da[u][:].rearrange("p t j -> p j t"))
+            da_words[u] = held.tile([P, last - first, PACK], BF16, name=f"da_words{u}", tag=tag, align_bytes=64)
+            copy(
+                da_words[u][:].rearrange("p (c i) t -> p c t i", i=LINE),
+                da(first, last).rearrange("p t (c i) -> p c t i", i=LINE),
+            )
 
         def quantise(u):
             first, last = UNITS[u]
@@ -196,13 +203,15 @@ def tile_moe_seb_none_kernel(
                 out=codes[u][:].bitcast(FP8X4), scales=code_s[u][:], in_=da_words[u][:].rearrange("p j t -> p (j t)")
             )
 
-        def multiply_w1(u, bank):
+        results = held.tile([P, KP, T], F32, name="results")
+
+        def multiply_w1(copy, u, h0, h1, bank):
             first, last = UNITS[u]
             e = first // C1
-            acc = psum.tile([P, KP, last - first], F32, name="acc1", tag=f"bank{bank}")
-            for h in range(KP):
+            acc = psum.tile([P, h1 - h0, last - first], F32, name="acc1", tag=f"bank{bank}")
+            for h in range(h0, h1):
                 nc.tensor.matmul_mx(
-                    out=acc[:, h, :],
+                    out=acc[:, h - h0, :],
                     lhsT=w1_w[:, e, 2 * P * h : 2 * P * (h + 1)].bitcast(FP4X4),
                     lhsT_scale=w1_s[:, e, h * P : (h + 1) * P],
                     rhs=codes[u][:].bitcast(FP8X4),
@@ -210,45 +219,35 @@ def tile_moe_seb_none_kernel(
                     start=True,
                     stop=True,
                 )
-            results[u] = held.tile([P, KP, last - first], F32, name=f"results{u}")
-            on_scalar(results[u][:], acc[:])
+            copy(results[:, h0:h1, first:last], acc[:])
 
         dx = [held.tile([P, T], F32, name=f"dx{h}") for h in range(KP)]
 
-        def scatter_dx(copy, u, h):
-            copy(dx[h][:].indirect(entries(list1, *UNITS[u])), results[u][:, h, :])
+        def scatter_dx(copy, h, first, last):
+            copy(dx[h][:].indirect(entries(list1, first, last)), results[:, h, first:last])
 
-        gather_dc(0, 0)
-        scatter_dc(on_vector, 2, 4, 6)
-        for u in range(1, 4):
-            gather_dc(0, u)
-        for t in (1, 2):
-            for u in range(4):
-                gather_dc(t, u)
-        gather_dc(3, 0)
-        gather_dc(3, 1)
-        round_da(on_vector, 0)
-        gather_dc(3, 2)
-        round_da(on_scalar, 1)
+        for t in range(PACK - 1):
+            gather_dc(t, 0, C1)
+            gather_dc(t, C1, T)
+        for u in range(4):
+            gather_dc(3, *UNITS[u])
+        for u in range(3):
+            round_da(on_scalar, u, f"da_words{u}")
         quantise(0)
-        round_da(on_scalar, 2)
-        gather_dc(3, 3)
-        multiply_w1(0, 7)
         quantise(1)
-        scatter_dx(on_scalar, 0, 1)
-        round_da(on_vector, 3)
-        multiply_w1(1, 0)
+        round_da(on_vector, 3, "da_first")
         quantise(2)
-        scatter_dx(on_vector, 0, 0)
-        scatter_dx(on_scalar, 1, 1)
-        multiply_w1(2, 1)
         quantise(3)
-        scatter_dx(on_vector, 1, 0)
-        scatter_dx(on_scalar, 2, 1)
-        multiply_w1(3, 2)
-        scatter_dx(on_vector, 2, 0)
-        scatter_dx(on_scalar, 3, 1)
-        scatter_dx(on_vector, 3, 0)
+        multiply_w1(on_scalar, 0, 0, KP, 7)
+        multiply_w1(on_scalar, 1, 0, KP, 0)
+        scatter_dx(on_vector, 0, 0, C1)
+        scatter_dx(on_scalar, 1, *UNITS[0])
+        multiply_w1(on_scalar, 2, 0, KP, 1)
+        scatter_dx(on_scalar, 1, *UNITS[1])
+        multiply_w1(on_scalar, 3, 0, KP, 2)
+        scatter_dx(on_scalar, 1, *UNITS[2])
+        scatter_dx(on_scalar, 1, *UNITS[3])
+        scatter_dx(on_vector, 0, C1, T)
 
         for h in range(KP):
             nc.sync.dma_start(out=out[h * P : (h + 1) * P, :], in_=dx[h][:])

@@ -22,7 +22,7 @@ LIST = 16
 PACK = 4
 LINE = 4
 KP = K // P
-UNITS = ((0, 128), (128, 256), (256, 512), (512, 768))
+UNITS = ((0, 128), (128, 384), (384, 768))
 
 
 def entries(offsets, first, last):
@@ -172,17 +172,18 @@ def tile_moe_seb_none_kernel(
         for f in (2, 4):
             for t in (1, 2):
                 scatter_dc(on_scalar, t, f, f + 2)
-        scatter_dc(on_scalar, 3, 3, 6)
+        scatter_dc(on_vector, 3, 5, 6)
+        scatter_dc(on_scalar, 3, 3, 5)
 
-        da_first = held.tile([P, PACK, C1], F32, name="da_first", tag="da_first", align_bytes=64)
-        da_rest = held.tile([P, PACK, T - C1], F32, name="da_rest")
+        da = [
+            held.tile([P, PACK, last - first], F32, name=f"da{u}", tag=f"da{u}", align_bytes=64)
+            for u, (first, last) in enumerate(UNITS)
+        ]
 
-        def da(first, last):
-            return da_first[:, :, first:last] if first < C1 else da_rest[:, :, first - C1 : last - C1]
-
-        def gather_dc(t, first, last):
+        def gather_dc(t, u):
+            first, last = UNITS[u]
             nc.vector.tensor_tensor(
-                da(first, last)[:, t, :], dc[t][:].indirect(entries(list1, first, last)), g_rows[:, first:last], MULT
+                da[u][:, t, :], dc[t][:].indirect(entries(list1, first, last)), g_rows[:, first:last], MULT
             )
 
         da_words, codes, code_s = {}, {}, {}
@@ -192,7 +193,7 @@ def tile_moe_seb_none_kernel(
             da_words[u] = held.tile([P, last - first, PACK], BF16, name=f"da_words{u}", tag=tag, align_bytes=64)
             copy(
                 da_words[u][:].rearrange("p (c i) t -> p c t i", i=LINE),
-                da(first, last).rearrange("p t (c i) -> p c t i", i=LINE),
+                da[u][:].rearrange("p t (c i) -> p c t i", i=LINE),
             )
 
         def quantise(u):
@@ -207,18 +208,19 @@ def tile_moe_seb_none_kernel(
 
         def multiply_w1(copy, u, h0, h1, bank):
             first, last = UNITS[u]
-            e = first // C1
             acc = psum.tile([P, h1 - h0, last - first], F32, name="acc1", tag=f"bank{bank}")
             for h in range(h0, h1):
-                nc.tensor.matmul_mx(
-                    out=acc[:, h - h0, :],
-                    lhsT=w1_w[:, e, 2 * P * h : 2 * P * (h + 1)].bitcast(FP4X4),
-                    lhsT_scale=w1_s[:, e, h * P : (h + 1) * P],
-                    rhs=codes[u][:].bitcast(FP8X4),
-                    rhs_scale=code_s[u][:],
-                    start=True,
-                    stop=True,
-                )
+                for e in range(first // C1, (last - 1) // C1 + 1):
+                    own = slice(max(first, e * C1) - first, min(last, (e + 1) * C1) - first)
+                    nc.tensor.matmul_mx(
+                        out=acc[:, h - h0, own],
+                        lhsT=w1_w[:, e, 2 * P * h : 2 * P * (h + 1)].bitcast(FP4X4),
+                        lhsT_scale=w1_s[:, e, h * P : (h + 1) * P],
+                        rhs=codes[u][:, own].bitcast(FP8X4),
+                        rhs_scale=code_s[u][:, own],
+                        start=True,
+                        stop=True,
+                    )
             copy(results[:, h0:h1, first:last], acc[:])
 
         dx = [held.tile([P, T], F32, name=f"dx{h}") for h in range(KP)]
@@ -226,28 +228,25 @@ def tile_moe_seb_none_kernel(
         def scatter_dx(copy, h, first, last):
             copy(dx[h][:].indirect(entries(list1, first, last)), results[:, h, first:last])
 
-        for t in range(PACK - 1):
-            gather_dc(t, 0, C1)
-            gather_dc(t, C1, T)
-        for u in range(4):
-            gather_dc(3, *UNITS[u])
-        for u in range(3):
-            round_da(on_scalar, u, f"da_words{u}")
+        for t in range(PACK):
+            for u in range(len(UNITS)):
+                gather_dc(t, u)
+        round_da(on_scalar, 0, "da_words0")
+        round_da(on_scalar, 1, "da_words1")
         quantise(0)
+        round_da(on_vector, 2, "da0")
         quantise(1)
-        round_da(on_vector, 3, "da_first")
         quantise(2)
-        quantise(3)
         multiply_w1(on_scalar, 0, 0, KP, 7)
-        multiply_w1(on_scalar, 1, 0, KP, 0)
-        scatter_dx(on_vector, 0, 0, C1)
+        scatter_dx(on_vector, 0, *UNITS[0])
         scatter_dx(on_scalar, 1, *UNITS[0])
-        multiply_w1(on_scalar, 2, 0, KP, 1)
+        multiply_w1(on_scalar, 1, 0, KP, 0)
+        multiply_w1(on_vector, 2, 0, 1, 1)
+        scatter_dx(on_vector, 0, *UNITS[1])
         scatter_dx(on_scalar, 1, *UNITS[1])
-        multiply_w1(on_scalar, 3, 0, KP, 2)
+        multiply_w1(on_scalar, 2, 1, 2, 0)
+        scatter_dx(on_vector, 0, *UNITS[2])
         scatter_dx(on_scalar, 1, *UNITS[2])
-        scatter_dx(on_scalar, 1, *UNITS[3])
-        scatter_dx(on_vector, 0, C1, T)
 
         for h in range(KP):
             nc.sync.dma_start(out=out[h * P : (h + 1) * P, :], in_=dx[h][:])

@@ -172,8 +172,7 @@ def tile_moe_seb_none_kernel(
         for f in (2, 4):
             for t in (1, 2):
                 scatter_dc(on_scalar, t, f, f + 2)
-        scatter_dc(on_vector, 3, 5, 6)
-        scatter_dc(on_scalar, 3, 3, 5)
+        scatter_dc(on_scalar, 3, 3, 6)
 
         da = [
             held.tile([P, PACK, last - first], F32, name=f"da{u}", tag=f"da{u}", align_bytes=64)

@@ -21,6 +21,7 @@ P = 128
 LIST = 16
 PACK = 4
 LINE = 4
+SHARE = 160
 KP = K // P
 UNITS = ((0, 128), (128, 384), (384, 768))
 
@@ -64,7 +65,7 @@ def tile_moe_seb_none_kernel(
         w2_w = {}
 
         def load_w2_words(f0, f1):
-            tile = held.tile([P, f1 - f0, H], U32, name=f"w2_w{f0}", align_bytes=64)
+            tile = held.tile([P, f1 - f0, H], U32, name=f"w2_w{f0}", tag=f"w2_w{f0}", align_bytes=64)
             src = w2t_words[f0:f1, 0].rearrange("f p i d -> p f (i d)")
             nc.sync.dma_start(out=tile[:].bitcast(I32), in_=src.bitcast(I32))
             for f in range(f0, f1):
@@ -81,10 +82,13 @@ def tile_moe_seb_none_kernel(
         load_w2_scales(0, 4)
         load_w2_words(1, 2)
         load_q_rows(0, 2)
-        load_w2_words(2, 4)
-        load_w2_words(4, E2)
+        load_w2_words(2, 3)
+        load_q_rows(2, 4)
+        load_w2_words(3, 4)
         load_w2_scales(4, E2)
-        load_q_rows(2, E2)
+        load_w2_words(4, 5)
+        load_w2_words(5, E2)
+        load_q_rows(4, E2)
         nc.sync.dma_start(out=g_rows[:], in_=gate1)
         nc.sync.dma_start(list1[:], offs)
         w1_rows = w1t_scales[:, 0].rearrange("e (q r) k -> r q e k", r=4)
@@ -95,7 +99,7 @@ def tile_moe_seb_none_kernel(
         slot_w, slot_s = {}, {}
 
         def gather_slots(table, dtype, by_expert, f0, f1, tag):
-            tile = held.tile([P, (f1 - f0) * C2], dtype, name=tag, tag=tag, align_bytes=64)
+            tile = held.tile([P, (f1 - f0) * C2], dtype, name=f"slots_{tag}", tag=tag, align_bytes=64)
             nc.vector.tensor_copy(tile[:], table[:].indirect(entries(list2, f0 * C2, f1 * C2)))
             for f in range(f0, f1):
                 by_expert[f] = tile[:, (f - f0) * C2 : (f - f0 + 1) * C2]
@@ -130,8 +134,9 @@ def tile_moe_seb_none_kernel(
                     start=True,
                     stop=True,
                 )
-            gate = q_rows[:, f * C2 : (f + 1) * C2].unsqueeze(1).to_broadcast([P, t1 - t0, C2])
-            nc.vector.tensor_tensor(sums[:, t0:t1, f * C2 : (f + 1) * C2], acc[:], gate, MULT)
+            for a, b in ((0, 1), (1, PACK)) if f in (1, E2 - 1) else ((t0, t1),):
+                gate = q_rows[:, f * C2 : (f + 1) * C2].unsqueeze(1).to_broadcast([P, b - a, C2])
+                nc.vector.tensor_tensor(sums[:, a:b, f * C2 : (f + 1) * C2], acc[:, a - t0 : b - t0, :], gate, MULT)
 
         dc = [held.tile([P, T], F32, name=f"dc{t}") for t in range(PACK)]
 
@@ -140,8 +145,11 @@ def tile_moe_seb_none_kernel(
 
         on_vector = nc.vector.tensor_copy
 
+        def scatter_slots(copy, t, first, last):
+            copy(dc[t][:].indirect(entries(list2, first, last)), sums[:, t, first:last])
+
         def scatter_dc(copy, t, f0, f1):
-            copy(dc[t][:].indirect(entries(list2, f0 * C2, f1 * C2)), sums[:, t, f0 * C2 : f1 * C2])
+            scatter_slots(copy, t, f0 * C2, f1 * C2)
 
         gather_slots(dy_s, U8, slot_s, 0, 4, "slot_s0")
         gather_slots(dy_w, U32, slot_w, 0, 1, "slot_w0")
@@ -153,26 +161,26 @@ def tile_moe_seb_none_kernel(
         reorder_words(nc.scalar.copy, 1, 0, PACK)
         multiply_w2(0, 0, 2, 0)
         multiply_w2(0, 2, 4, 1)
-        multiply_w2(1, 0, 4, 2)
-        for f in range(2, 5):
+        for f in range(2, E2):
+            if f == 4:
+                reorder_scales(1, 0, PACK)
             reorder_words(nc.gpsimd.tensor_copy, f, 0, PACK)
-        reorder_scales(1, 0, PACK)
-        reorder_words(nc.gpsimd.tensor_copy, 5, 0, PACK)
-        scatter_dc(on_vector, 0, 0, 1)
-        gather_slots(dy_s, U8, slot_s, 4, 6, "slot_w1")
+        gather_slots(dy_s, U8, slot_s, 4, 6, "w2_w1")
+        for t in range(PACK - 1):
+            scatter_dc(on_scalar, t, 0, 1)
+        multiply_w2(1, 0, 4, 2)
+        scatter_dc(on_vector, 0, 1, 2)
         gather_slots(dy_w, U32, slot_w, 4, 6, "plane_w1_0")
         multiply_w2(2, 0, 4, 3)
         multiply_w2(3, 0, 4, 4)
-        scatter_dc(on_vector, 0, 1, 3)
+        scatter_dc(on_vector, 0, 2, 3)
         multiply_w2(4, 0, 4, 5)
         multiply_w2(5, 0, 4, 6)
         scatter_dc(on_vector, 0, 3, 6)
-        for t, f0, f1 in ((1, 0, 1), (2, 0, 1), (3, 0, 1), (1, 1, 2), (2, 1, 2), (3, 1, 3)):
+        for t, f0, f1 in ((1, 1, 2), (2, 1, 2), (3, 0, 2), (1, 2, 4), (2, 2, 4), (1, 4, 6), (2, 4, 6)):
             scatter_dc(on_scalar, t, f0, f1)
-        for f in (2, 4):
-            for t in (1, 2):
-                scatter_dc(on_scalar, t, f, f + 2)
-        scatter_dc(on_scalar, 3, 3, 6)
+        scatter_slots(on_vector, 3, T - SHARE, T)
+        scatter_slots(on_scalar, 3, 2 * C2, T - SHARE)
 
         da = [
             held.tile([P, PACK, last - first], F32, name=f"da{u}", tag=f"da{u}", align_bytes=64)
@@ -228,7 +236,7 @@ def tile_moe_seb_none_kernel(
             copy(dx[h][:].indirect(entries(list1, first, last)), results[:, h, first:last])
 
         for t in range(PACK):
-            for u in range(len(UNITS)):
+            for u in range(len(UNITS)) if t else reversed(range(len(UNITS))):
                 gather_dc(t, u)
         round_da(on_scalar, 0, "da_words0")
         round_da(on_scalar, 1, "da_words1")

@@ -21,7 +21,7 @@ P = 128
 LIST = 16
 PACK = 4
 LINE = 4
-SHARE = 160
+SHARE = 192
 KP = K // P
 UNITS = ((0, 128), (128, 384), (384, 768))
 
@@ -155,6 +155,7 @@ def tile_moe_seb_none_kernel(
         gather_slots(dy_w, U32, slot_w, 0, 1, "slot_w0")
         gather_slots(dy_w, U32, slot_w, 1, 2, "slot_w1")
         gather_slots(dy_w, U32, slot_w, 2, 4, "slot_w2")
+        gather_slots(dy_s, U8, slot_s, 4, 6, "slot_s4")
         for t0 in (0, 2):
             reorder_words(nc.scalar.copy, 0, t0, t0 + 2)
             reorder_scales(0, t0, t0 + 2)
@@ -165,12 +166,11 @@ def tile_moe_seb_none_kernel(
             if f == 4:
                 reorder_scales(1, 0, PACK)
             reorder_words(nc.gpsimd.tensor_copy, f, 0, PACK)
-        gather_slots(dy_s, U8, slot_s, 4, 6, "w2_w1")
+        gather_slots(dy_w, U32, slot_w, 4, 6, "w2_w1")
         for t in range(PACK - 1):
             scatter_dc(on_scalar, t, 0, 1)
         multiply_w2(1, 0, 4, 2)
         scatter_dc(on_vector, 0, 1, 2)
-        gather_slots(dy_w, U32, slot_w, 4, 6, "plane_w1_0")
         multiply_w2(2, 0, 4, 3)
         multiply_w2(3, 0, 4, 4)
         scatter_dc(on_vector, 0, 2, 3)

@@ -22,6 +22,7 @@ LIST = 16
 PACK = 4
 LINE = 4
 SHARE = 192
+HELP = 64
 KP = K // P
 UNITS = ((0, 128), (128, 384), (384, 768))
 
@@ -195,65 +196,74 @@ def tile_moe_seb_none_kernel(
 
         da_words, codes, code_s = {}, {}, {}
 
-        def round_da(copy, u, tag):
-            first, last = UNITS[u]
-            da_words[u] = held.tile([P, last - first, PACK], BF16, name=f"da_words{u}", tag=tag, align_bytes=64)
+        def round_da(copy, u, first, last):
+            part = slice(first - UNITS[u][0], last - UNITS[u][0])
             copy(
-                da_words[u][:].rearrange("p (c i) t -> p c t i", i=LINE),
-                da[u][:].rearrange("p t (c i) -> p c t i", i=LINE),
+                da_words[u][:, part, :].rearrange("p (c i) t -> p c t i", i=LINE),
+                da[u][:, :, part].rearrange("p t (c i) -> p c t i", i=LINE),
             )
 
-        def quantise(u):
+        def words_tile(u, tag):
+            first, last = UNITS[u]
+            da_words[u] = held.tile([P, last - first, PACK], BF16, name=f"da_words{u}", tag=tag, align_bytes=64)
+
+        def quantise(u, scales_tag):
             first, last = UNITS[u]
             codes[u] = held.tile([P, last - first], U32, name=f"codes{u}", align_bytes=64)
-            code_s[u] = held.tile([P, last - first], U8, name=f"code_s{u}", align_bytes=64)
+            code_s[u] = held.tile([P, last - first], U8, name=f"code_s{u}", tag=scales_tag, align_bytes=64)
             nc.vector.quantize_mx(
                 out=codes[u][:].bitcast(FP8X4), scales=code_s[u][:], in_=da_words[u][:].rearrange("p j t -> p (j t)")
             )
 
-        results = held.tile([P, KP, T], F32, name="results")
+        results = {}
 
-        def multiply_w1(copy, u, h0, h1, bank):
+        def multiply_w1(copy, u, h, bank):
             first, last = UNITS[u]
-            acc = psum.tile([P, h1 - h0, last - first], F32, name="acc1", tag=f"bank{bank}")
-            for h in range(h0, h1):
-                for e in range(first // C1, (last - 1) // C1 + 1):
-                    own = slice(max(first, e * C1) - first, min(last, (e + 1) * C1) - first)
-                    nc.tensor.matmul_mx(
-                        out=acc[:, h - h0, own],
-                        lhsT=w1_w[:, e, 2 * P * h : 2 * P * (h + 1)].bitcast(FP4X4),
-                        lhsT_scale=w1_s[:, e, h * P : (h + 1) * P],
-                        rhs=codes[u][:, own].bitcast(FP8X4),
-                        rhs_scale=code_s[u][:, own],
-                        start=True,
-                        stop=True,
-                    )
-            copy(results[:, h0:h1, first:last], acc[:])
+            acc = psum.tile([P, last - first], F32, name="acc1", tag=f"bank{bank}")
+            for e in range(first // C1, (last - 1) // C1 + 1):
+                own = slice(max(first, e * C1) - first, min(last, (e + 1) * C1) - first)
+                nc.tensor.matmul_mx(
+                    out=acc[:, own],
+                    lhsT=w1_w[:, e, 2 * P * h : 2 * P * (h + 1)].bitcast(FP4X4),
+                    lhsT_scale=w1_s[:, e, h * P : (h + 1) * P],
+                    rhs=codes[u][:, own].bitcast(FP8X4),
+                    rhs_scale=code_s[u][:, own],
+                    start=True,
+                    stop=True,
+                )
+            name = f"results{u}_{h}"
+            results[u, h] = held.tile([P, last - first], F32, name=name, tag=name, align_bytes=64)
+            copy(results[u, h][:], acc[:])
 
         dx = [held.tile([P, T], F32, name=f"dx{h}") for h in range(KP)]
 
-        def scatter_dx(copy, h, first, last):
-            copy(dx[h][:].indirect(entries(list1, first, last)), results[:, h, first:last])
+        def scatter_dx(copy, h, u):
+            copy(dx[h][:].indirect(entries(list1, *UNITS[u])), results[u, h][:])
 
         for t in range(PACK):
             for u in range(len(UNITS)) if t else reversed(range(len(UNITS))):
                 gather_dc(t, u)
-        round_da(on_scalar, 0, "da_words0")
-        round_da(on_scalar, 1, "da_words1")
-        quantise(0)
-        round_da(on_vector, 2, "da0")
-        quantise(1)
-        quantise(2)
-        multiply_w1(on_scalar, 0, 0, KP, 7)
-        scatter_dx(on_vector, 0, *UNITS[0])
-        scatter_dx(on_scalar, 1, *UNITS[0])
-        multiply_w1(on_scalar, 1, 0, KP, 0)
-        multiply_w1(on_vector, 2, 0, 1, 1)
-        scatter_dx(on_vector, 0, *UNITS[1])
-        scatter_dx(on_scalar, 1, *UNITS[1])
-        multiply_w1(on_scalar, 2, 1, 2, 0)
-        scatter_dx(on_vector, 0, *UNITS[2])
-        scatter_dx(on_scalar, 1, *UNITS[2])
+        for u, tag in enumerate(("da_words0", "da_words1")):
+            words_tile(u, tag)
+            round_da(on_scalar, u, *UNITS[u])
+        words_tile(2, "da0")
+        round_da(on_scalar, 2, UNITS[2][0], UNITS[2][0] + HELP)
+        quantise(0, "code_s0")
+        round_da(on_vector, 2, UNITS[2][0] + HELP, T)
+        quantise(1, "code_s1")
+        multiply_w1(on_scalar, 0, 1, 7)
+        multiply_w1(on_scalar, 0, 0, 0)
+        scatter_dx(on_vector, 0, 0)
+        scatter_dx(on_scalar, 1, 0)
+        quantise(2, "results0_1")
+        multiply_w1(on_scalar, 1, 1, 1)
+        multiply_w1(on_scalar, 1, 0, 2)
+        scatter_dx(on_vector, 0, 1)
+        scatter_dx(on_scalar, 1, 1)
+        multiply_w1(on_scalar, 2, 0, 3)
+        multiply_w1(on_vector, 2, 1, 4)
+        scatter_dx(on_vector, 0, 2)
+        scatter_dx(on_scalar, 1, 2)
 
         for h in range(KP):
             nc.sync.dma_start(out=out[h * P : (h + 1) * P, :], in_=dx[h][:])

@@ -21,9 +21,10 @@ P = 128
 LIST = 16
 PACK = 4
 LINE = 4
-SHARE = 192
+SHARE = 224
 HELP = 64
 KP = K // P
+SPARE = 32
 UNITS = ((0, 128), (128, 384), (384, 768))
 
 
@@ -100,7 +101,7 @@ def tile_moe_seb_none_kernel(
         slot_w, slot_s = {}, {}
 
         def gather_slots(table, dtype, by_expert, f0, f1, tag):
-            tile = held.tile([P, (f1 - f0) * C2], dtype, name=f"slots_{tag}", tag=tag, align_bytes=64)
+            tile = held.tile([P, (f1 - f0) * C2], dtype, name=f"slots_{tag}", tag=tag, align_bytes=64)[:]
             nc.vector.tensor_copy(tile[:], table[:].indirect(entries(list2, f0 * C2, f1 * C2)))
             for f in range(f0, f1):
                 by_expert[f] = tile[:, (f - f0) * C2 : (f - f0 + 1) * C2]
@@ -135,11 +136,13 @@ def tile_moe_seb_none_kernel(
                     start=True,
                     stop=True,
                 )
-            for a, b in ((0, 1), (1, PACK)) if f in (1, E2 - 1) else ((t0, t1),):
+            for a, b in ((0, 1), (1, PACK)) if f in (3, E2 - 1) else ((t0, t1),):
                 gate = q_rows[:, f * C2 : (f + 1) * C2].unsqueeze(1).to_broadcast([P, b - a, C2])
                 nc.vector.tensor_tensor(sums[:, a:b, f * C2 : (f + 1) * C2], acc[:, a - t0 : b - t0, :], gate, MULT)
 
-        dc = [held.tile([P, T], F32, name=f"dc{t}") for t in range(PACK)]
+        dc = [held.tile([P, T + SPARE * (t < PACK - 1)], F32, name=f"dc{t}") for t in range(PACK)]
+        for t in range(PACK - 1):
+            nc.gpsimd.memset(dc[t][:, T:], 0.0)
 
         def on_scalar(dst, src):
             nc.scalar.activation(dst, src, COPY)
@@ -154,8 +157,7 @@ def tile_moe_seb_none_kernel(
 
         gather_slots(dy_s, U8, slot_s, 0, 4, "slot_s0")
         gather_slots(dy_w, U32, slot_w, 0, 1, "slot_w0")
-        gather_slots(dy_w, U32, slot_w, 1, 2, "slot_w1")
-        gather_slots(dy_w, U32, slot_w, 2, 4, "slot_w2")
+        gather_slots(dy_w, U32, slot_w, 1, 4, "slot_w1")
         gather_slots(dy_s, U8, slot_s, 4, 6, "slot_s4")
         for t0 in (0, 2):
             reorder_words(nc.scalar.copy, 0, t0, t0 + 2)
@@ -171,27 +173,24 @@ def tile_moe_seb_none_kernel(
         for t in range(PACK - 1):
             scatter_dc(on_scalar, t, 0, 1)
         multiply_w2(1, 0, 4, 2)
-        scatter_dc(on_vector, 0, 1, 2)
         multiply_w2(2, 0, 4, 3)
         multiply_w2(3, 0, 4, 4)
-        scatter_dc(on_vector, 0, 2, 3)
+        scatter_dc(on_vector, 0, 1, 4)
         multiply_w2(4, 0, 4, 5)
         multiply_w2(5, 0, 4, 6)
-        scatter_dc(on_vector, 0, 3, 6)
-        for t, f0, f1 in ((1, 1, 2), (2, 1, 2), (3, 0, 2), (1, 2, 4), (2, 2, 4), (1, 4, 6), (2, 4, 6)):
+        scatter_dc(on_vector, 0, 4, 6)
+        for t, f0, f1 in ((3, 0, 2), (1, 1, 3), (2, 1, 3), (1, 3, 6), (2, 3, 6)):
             scatter_dc(on_scalar, t, f0, f1)
         scatter_slots(on_vector, 3, T - SHARE, T)
         scatter_slots(on_scalar, 3, 2 * C2, T - SHARE)
 
-        da = [
-            held.tile([P, PACK, last - first], F32, name=f"da{u}", tag=f"da{u}", align_bytes=64)
-            for u, (first, last) in enumerate(UNITS)
-        ]
+        wide = UNITS[2][1] - UNITS[2][0]
+        room = held.tile([P, 2 * wide - P + PACK * T], F32, name="room", align_bytes=64)
+        da = room[:, 2 * wide - P :].rearrange("p (t j) -> p t j", t=PACK)
 
-        def gather_dc(t, u):
-            first, last = UNITS[u]
+        def gather_dc(t, first, last):
             nc.vector.tensor_tensor(
-                da[u][:, t, :], dc[t][:].indirect(entries(list1, first, last)), g_rows[:, first:last], MULT
+                da[:, t, first:last], dc[t][:].indirect(entries(list1, first, last)), g_rows[:, first:last], MULT
             )
 
         da_words, codes, code_s = {}, {}, {}
@@ -200,7 +199,7 @@ def tile_moe_seb_none_kernel(
             part = slice(first - UNITS[u][0], last - UNITS[u][0])
             copy(
                 da_words[u][:, part, :].rearrange("p (c i) t -> p c t i", i=LINE),
-                da[u][:, :, part].rearrange("p t (c i) -> p c t i", i=LINE),
+                da[:, :, first:last].rearrange("p t (c i) -> p c t i", i=LINE),
             )
 
         def words_tile(u, tag):
@@ -212,7 +211,7 @@ def tile_moe_seb_none_kernel(
             codes[u] = held.tile([P, last - first], U32, name=f"codes{u}", align_bytes=64)
             code_s[u] = held.tile([P, last - first], U8, name=f"code_s{u}", tag=scales_tag, align_bytes=64)
             nc.vector.quantize_mx(
-                out=codes[u][:].bitcast(FP8X4), scales=code_s[u][:], in_=da_words[u][:].rearrange("p j t -> p (j t)")
+                out=codes[u][:].bitcast(FP8X4), scales=code_s[u][:], in_=da_words[u].rearrange("p j t -> p (j t)")
             )
 
         results = {}
@@ -240,13 +239,14 @@ def tile_moe_seb_none_kernel(
         def scatter_dx(copy, h, u):
             copy(dx[h][:].indirect(entries(list1, *UNITS[u])), results[u, h][:])
 
-        for t in range(PACK):
-            for u in range(len(UNITS)) if t else reversed(range(len(UNITS))):
-                gather_dc(t, u)
+        for t in range(PACK - 1):
+            gather_dc(t, 0, T)
+        for first, last in UNITS:
+            gather_dc(PACK - 1, first, last)
         for u, tag in enumerate(("da_words0", "da_words1")):
             words_tile(u, tag)
             round_da(on_scalar, u, *UNITS[u])
-        words_tile(2, "da0")
+        da_words[2] = room[:, : 2 * wide].bitcast(BF16).rearrange("p (j t) -> p j t", t=PACK)
         round_da(on_scalar, 2, UNITS[2][0], UNITS[2][0] + HELP)
         quantise(0, "code_s0")
         round_da(on_vector, 2, UNITS[2][0] + HELP, T)
@@ -261,7 +261,7 @@ def tile_moe_seb_none_kernel(
         scatter_dx(on_vector, 0, 1)
         scatter_dx(on_scalar, 1, 1)
         multiply_w1(on_scalar, 2, 0, 3)
-        multiply_w1(on_vector, 2, 1, 4)
+        multiply_w1(on_scalar, 2, 1, 4)
         scatter_dx(on_vector, 0, 2)
         scatter_dx(on_scalar, 1, 2)
 

@@ -21,8 +21,9 @@ P = 128
 LIST = 16
 PACK = 4
 LINE = 4
-SHARE = 224
+SHARE = 256
 HELP = 64
+LONG = 384
 KP = K // P
 SPARE = 32
 UNITS = ((0, 128), (128, 384), (384, 768))
@@ -179,10 +180,11 @@ def tile_moe_seb_none_kernel(
         multiply_w2(4, 0, 4, 5)
         multiply_w2(5, 0, 4, 6)
         scatter_dc(on_vector, 0, 4, 6)
-        for t, f0, f1 in ((3, 0, 2), (1, 1, 3), (2, 1, 3), (1, 3, 6), (2, 3, 6)):
+        scatter_slots(on_scalar, 3, 0, T - SHARE - LONG)
+        for t, f0, f1 in ((1, 1, 3), (2, 1, 3), (1, 3, 6), (2, 3, 6)):
             scatter_dc(on_scalar, t, f0, f1)
         scatter_slots(on_vector, 3, T - SHARE, T)
-        scatter_slots(on_scalar, 3, 2 * C2, T - SHARE)
+        scatter_slots(on_scalar, 3, T - SHARE - LONG, T - SHARE)
 
         wide = UNITS[2][1] - UNITS[2][0]
         room = held.tile([P, 2 * wide - P + PACK * T], F32, name="room", align_bytes=64)

from contextlib import ExitStack

import concourse.mybir as mybir

K, T, H, N = 256, 768, 512, 512
E1, C1, E2, C2 = 3, 256, 6, 128
FLOPS = 2 * T * (N * H + H * K)

F32 = mybir.dt.float32
BF16 = mybir.dt.bfloat16
I32 = mybir.dt.int32
U32 = mybir.dt.uint32
U16 = mybir.dt.uint16
U8 = mybir.dt.uint8
FP8X4 = mybir.dt.float8_e4m3fn_x4
FP4X4 = mybir.dt.float4_e2m1fn_x4
COPY = mybir.ActivationFunctionType.Copy
MULT = mybir.AluOpType.mult

P = 128
LIST = 16
PACK = 4
LINE = 4
SHARE = 256
HELP = 64
LONG = 384
KP = K // P
SPARE = 32
UNITS = ((0, 128), (128, 384), (384, 768))


def entries(offsets, first, last):
    return offsets[:, first // LIST : last // LIST]


def tile_moe_seb_none_kernel(
    tc, dy_words, dy_scales, w2t_words, w2t_scales, w1t_words, w1t_scales, gate1, gate2, offs, offs2, out
):
    nc = tc.nc
    with ExitStack() as ctx:
        held = ctx.enter_context(tc.tile_pool(name="held", bufs=1))
        psum = ctx.enter_context(tc.psum_pool(name="psum", bufs=1))

        list2 = held.tile([P, T // LIST], U16, name="list2")
        list1 = held.tile([P, T // LIST], U16, name="list1")
        dy_w = held.tile([P, T], U32, name="dy_w", align_bytes=64)
        dy_s = held.tile([P, T], U8, name="dy_s", align_bytes=64)
        w2_s = [held.tile([P, H], U8, name=f"w2_s{a}", align_bytes=64) for a in range(2)]
        w1_s = held.tile([P, E1, K], U8, name="w1_s", align_bytes=64)
        w1_w = held.tile([P, E1, 2 * K], U8, name="w1_w", align_bytes=64)
        q_rows = held.tile([P, T], F32, name="q_rows")
        g_rows = held.tile([P, T], F32, name="g_rows")

        nc.vector.memset(w2_s[0][:].bitcast(I32), 0)
        nc.vector.memset(w2_s[1][:].bitcast(I32), 0)
        nc.vector.memset(w1_s[:].bitcast(I32), 0)

        def load_w2_scales(f0, f1):
            for q in range(4):
                nc.sync.dma_start(
                    out=w2_s[f0 // 4][32 * q : 32 * q + 4 * (f1 - f0), :].bitcast(I32),
                    in_=w2t_scales[f0:f1, 0, 4 * q : 4 * q + 4, :].bitcast(I32),
                )

        def load_q_rows(f0, f1):
            nc.sync.dma_start(out=q_rows[:, f0 * C2 : f1 * C2], in_=gate2[:, f0 * C2 : f1 * C2])

        w2_w = {}

        def load_w2_words(f0, f1):
            tile = held.tile([P, f1 - f0, H], U32, name=f"w2_w{f0}", tag=f"w2_w{f0}", align_bytes=64)
            src = w2t_words[f0:f1, 0].rearrange("f p i d -> p f (i d)")
            nc.sync.dma_start(out=tile[:].bitcast(I32), in_=src.bitcast(I32))
            for f in range(f0, f1):
                w2_w[f] = tile[:, f - f0, :]

        nc.sync.dma_start(list2[:], offs2)
        for q in range(4):
            rows = dy_scales[0, 4 * q : 4 * q + 4, :].bitcast(I32)
            (nc.sync, nc.scalar)[q // 2].dma_start(
                out=dy_s[32 * q : 32 * q + 32, :].bitcast(I32), in_=rows.unsqueeze(0).to_broadcast([8, 4, T // 4])
            )
        nc.sync.dma_start(out=dy_w[:].bitcast(I32), in_=dy_words[0].rearrange("p t d -> p (t d)").bitcast(I32))
        load_w2_words(0, 1)
        load_w2_scales(0, 4)
        load_w2_words(1, 2)
        load_q_rows(0, 2)
        load_w2_words(2, 3)
        load_q_rows(2, 4)
        load_w2_words(3, 4)
        load_w2_scales(4, E2)
        load_w2_words(4, 5)
        load_w2_words(5, E2)
        load_q_rows(4, E2)
        nc.sync.dma_start(out=g_rows[:], in_=gate1)
        nc.sync.dma_start(list1[:], offs)
        w1_rows = w1t_scales[:, 0].rearrange("e (q r) k -> r q e k", r=4)
        for r in range(4):
            nc.sync.dma_start(out=w1_s[r:P:32].bitcast(I32), in_=w1_rows[r].bitcast(I32))
        nc.sync.dma_start(out=w1_w[:].bitcast(I32), in_=w1t_words[:, 0].rearrange("e p c -> p e c").bitcast(I32))

        slot_w, slot_s = {}, {}

        def gather_slots(table, dtype, by_expert, f0, f1, tag):
            tile = held.tile([P, (f1 - f0) * C2], dtype, name=f"slots_{tag}", tag=tag, align_bytes=64)[:]
            nc.vector.tensor_copy(tile[:], table[:].indirect(entries(list2, f0 * C2, f1 * C2)))
            for f in range(f0, f1):
                by_expert[f] = tile[:, (f - f0) * C2 : (f - f0 + 1) * C2]

        plane_w, plane_s = {}, {}

        def reorder_words(copy, f, t0, t1):
            tile = held.tile([P, t1 - t0, P], U32, name=f"plane_w{f}_{t0}", tag=f"plane_w{f}_{t0}", align_bytes=64)
            src = w2_w[f].rearrange("p (c i t) -> p c t i", i=LINE, t=PACK)[:, :, t0:t1, :]
            copy(tile[:].rearrange("p t (c i) -> p c t i", i=LINE), src)
            for t in range(t0, t1):
                plane_w[f, t] = tile[:, t - t0, :]

        def reorder_scales(a, t0, t1):
            tile = held.tile([P, t1 - t0, P], U8, name=f"plane_s{a}_{t0}", align_bytes=64)
            nc.gpsimd.tensor_copy(tile[:], w2_s[a][:].rearrange("p (m t) -> p t m", t=PACK)[:, t0:t1, :])
            for t in range(t0, t1):
                plane_s[a, t] = tile
                plane_s[a, t, "at"] = t - t0

        sums = held.tile([P, PACK, T], F32, name="sums")

        def multiply_w2(f, t0, t1, bank):
            acc = psum.tile([P, t1 - t0, C2], F32, name="acc2", tag=f"bank{bank}")
            for t in range(t0, t1):
                nc.tensor.matmul_mx(
                    out=acc[:, t - t0, :],
                    lhsT=plane_w[f, t].bitcast(FP8X4),
                    lhsT_scale=plane_s[f // 4, t][4 * (f % 4) :, plane_s[f // 4, t, "at"], :],
                    rhs=slot_w[f].bitcast(FP8X4),
                    rhs_scale=slot_s[f],
                    start=True,
                    stop=True,
                )
            for a, b in ((0, 1), (1, PACK)) if f in (3, E2 - 1) else ((t0, t1),):
                gate = q_rows[:, f * C2 : (f + 1) * C2].unsqueeze(1).to_broadcast([P, b - a, C2])
                nc.vector.tensor_tensor(sums[:, a:b, f * C2 : (f + 1) * C2], acc[:, a - t0 : b - t0, :], gate, MULT)

        dc = [held.tile([P, T + SPARE * (t < PACK - 1)], F32, name=f"dc{t}") for t in range(PACK)]
        for t in range(PACK - 1):
            nc.gpsimd.memset(dc[t][:, T:], 0.0)

        def on_scalar(dst, src):
            nc.scalar.activation(dst, src, COPY)

        on_vector = nc.vector.tensor_copy

        def scatter_slots(copy, t, first, last):
            copy(dc[t][:].indirect(entries(list2, first, last)), sums[:, t, first:last])

        def scatter_dc(copy, t, f0, f1):
            scatter_slots(copy, t, f0 * C2, f1 * C2)

        gather_slots(dy_s, U8, slot_s, 0, 4, "slot_s0")
        gather_slots(dy_w, U32, slot_w, 0, 1, "slot_w0")
        gather_slots(dy_w, U32, slot_w, 1, 4, "slot_w1")
        gather_slots(dy_s, U8, slot_s, 4, 6, "slot_s4")
        for t0 in (0, 2):
            reorder_words(nc.scalar.copy, 0, t0, t0 + 2)
            reorder_scales(0, t0, t0 + 2)
        reorder_words(nc.scalar.copy, 1, 0, PACK)
        multiply_w2(0, 0, 2, 0)
        multiply_w2(0, 2, 4, 1)
        for f in range(2, E2):
            if f == 4:
                reorder_scales(1, 0, PACK)
            reorder_words(nc.gpsimd.tensor_copy, f, 0, PACK)
        gather_slots(dy_w, U32, slot_w, 4, 6, "w2_w1")
        for t in range(PACK - 1):
            scatter_dc(on_scalar, t, 0, 1)
        multiply_w2(1, 0, 4, 2)
        multiply_w2(2, 0, 4, 3)
        multiply_w2(3, 0, 4, 4)
        scatter_dc(on_vector, 0, 1, 4)
        multiply_w2(4, 0, 4, 5)
        multiply_w2(5, 0, 4, 6)
        scatter_dc(on_vector, 0, 4, 6)
        scatter_slots(on_scalar, 3, 0, T - SHARE - LONG)
        for t, f0, f1 in ((1, 1, 3), (2, 1, 3), (1, 3, 6), (2, 3, 6)):
            scatter_dc(on_scalar, t, f0, f1)
        scatter_slots(on_vector, 3, T - SHARE, T)
        scatter_slots(on_scalar, 3, T - SHARE - LONG, T - SHARE)

        wide = UNITS[2][1] - UNITS[2][0]
        room = held.tile([P, 2 * wide - P + PACK * T], F32, name="room", align_bytes=64)
        da = room[:, 2 * wide - P :].rearrange("p (t j) -> p t j", t=PACK)

        def gather_dc(t, first, last):
            nc.vector.tensor_tensor(
                da[:, t, first:last], dc[t][:].indirect(entries(list1, first, last)), g_rows[:, first:last], MULT
            )

        da_words, codes, code_s = {}, {}, {}

        def round_da(copy, u, first, last):
            part = slice(first - UNITS[u][0], last - UNITS[u][0])
            copy(
                da_words[u][:, part, :].rearrange("p (c i) t -> p c t i", i=LINE),
                da[:, :, first:last].rearrange("p t (c i) -> p c t i", i=LINE),
            )

        def words_tile(u, tag):
            first, last = UNITS[u]
            da_words[u] = held.tile([P, last - first, PACK], BF16, name=f"da_words{u}", tag=tag, align_bytes=64)

        def quantise(u, scales_tag):
            first, last = UNITS[u]
            codes[u] = held.tile([P, last - first], U32, name=f"codes{u}", align_bytes=64)
            code_s[u] = held.tile([P, last - first], U8, name=f"code_s{u}", tag=scales_tag, align_bytes=64)
            nc.vector.quantize_mx(
                out=codes[u][:].bitcast(FP8X4), scales=code_s[u][:], in_=da_words[u].rearrange("p j t -> p (j t)")
            )

        results = {}

        def multiply_w1(copy, u, h, bank):
            first, last = UNITS[u]
            acc = psum.tile([P, last - first], F32, name="acc1", tag=f"bank{bank}")
            for e in range(first // C1, (last - 1) // C1 + 1):
                own = slice(max(first, e * C1) - first, min(last, (e + 1) * C1) - first)
                nc.tensor.matmul_mx(
                    out=acc[:, own],
                    lhsT=w1_w[:, e, 2 * P * h : 2 * P * (h + 1)].bitcast(FP4X4),
                    lhsT_scale=w1_s[:, e, h * P : (h + 1) * P],
                    rhs=codes[u][:, own].bitcast(FP8X4),
                    rhs_scale=code_s[u][:, own],
                    start=True,
                    stop=True,
                )
            name = f"results{u}_{h}"
            results[u, h] = held.tile([P, last - first], F32, name=name, tag=name, align_bytes=64)
            copy(results[u, h][:], acc[:])

        dx = [held.tile([P, T], F32, name=f"dx{h}") for h in range(KP)]

        def scatter_dx(copy, h, u):
            copy(dx[h][:].indirect(entries(list1, *UNITS[u])), results[u, h][:])

        for t in range(PACK - 1):
            gather_dc(t, 0, T)
        for first, last in UNITS:
            gather_dc(PACK - 1, first, last)
        for u, tag in enumerate(("da_words0", "da_words1")):
            words_tile(u, tag)
            round_da(on_scalar, u, *UNITS[u])
        da_words[2] = room[:, : 2 * wide].bitcast(BF16).rearrange("p (j t) -> p j t", t=PACK)
        round_da(on_scalar, 2, UNITS[2][0], UNITS[2][0] + HELP)
        quantise(0, "code_s0")
        round_da(on_vector, 2, UNITS[2][0] + HELP, T)
        quantise(1, "code_s1")
        multiply_w1(on_scalar, 0, 1, 7)
        multiply_w1(on_scalar, 0, 0, 0)
        scatter_dx(on_vector, 0, 0)
        scatter_dx(on_scalar, 1, 0)
        quantise(2, "results0_1")
        multiply_w1(on_scalar, 1, 1, 1)
        multiply_w1(on_scalar, 1, 0, 2)
        scatter_dx(on_vector, 0, 1)
        scatter_dx(on_scalar, 1, 1)
        multiply_w1(on_scalar, 2, 0, 3)
        multiply_w1(on_scalar, 2, 1, 4)
        scatter_dx(on_vector, 0, 2)
        scatter_dx(on_scalar, 1, 2)

        for h in range(KP):
            nc.sync.dma_start(out=out[h * P : (h + 1) * P, :], in_=dx[h][:])
